import numpy as np
import ml_dtypes


def mxq(x, axis, fmt="e4m3"):
    dtype, down = {"e4m3": (ml_dtypes.float8_e4m3fn, 7), "e5m2": (ml_dtypes.float8_e5m2, 14)}[fmt]
    v = np.moveaxis(np.asarray(x, np.float32).astype(ml_dtypes.bfloat16).astype(np.float64), axis, -1)
    blocks = v.reshape(v.shape[:-1] + (-1, 32))
    amax = np.abs(blocks).max(-1, keepdims=True)
    byte = np.maximum(np.where(amax > 0, np.frexp(amax)[1] - 1 + 127, 0) - down, 1)
    scale = np.exp2(byte - 127.0)
    codes = (blocks / scale).astype(np.float32).astype(dtype).astype(np.float64)
    return np.moveaxis((codes * scale).reshape(v.shape), -1, axis)


WIDE = False


def mx_kscale(k):
    if not WIDE:
        return np.ones(k)
    levels = np.array([10, -10, 5, -5, 0])
    if k % 512:
        return np.exp2(np.random.permutation(np.resize(levels, k // 32))).repeat(32)
    a = np.empty((k // 512, 16))
    for p in range(k // 512):
        a[p, :8] = np.random.permutation(np.resize(levels, 8))
        for g in range(8):
            far = levels[np.abs(levels - a[p, g]) >= 10]
            a[p, g + 8] = far[np.random.randint(len(far))]
    return np.exp2(a.ravel()).repeat(32)


def f64(x):
    return np.asarray(x).astype(np.float64)


def striped(idx):
    return np.tile(idx.reshape(-1, 16).T, (8, 1)).astype(np.uint16)


def unstriped(offs):
    return offs[:16].T.reshape(-1).astype(np.int64)


E2M1 = np.array([0.0, 0.5, 1.0, 1.5, 2.0, 3.0, 4.0, 6.0, -0.0, -0.5, -1.0, -1.5, -2.0, -3.0, -4.0, -6.0])


def pack_weight(w, fmt):
    k, n = w.shape
    w = f64(np.asarray(w, np.float32).astype(ml_dtypes.bfloat16)).reshape(k // 32, 32, n)
    amax = np.abs(w).max(1)
    if fmt == "e4m3":
        byte = np.frexp(amax)[1] - 1 + 127 - 7
    else:
        mant, ex = np.frexp(amax / 6.0)
        byte = np.where(mant > 0.5, ex, ex - 1) + 127
    byte = np.clip(np.where(amax > 0, byte, 1), 1, 254)
    scaled = (w * np.exp2(127.0 - byte)[:, None, :]).reshape(k, n).astype(np.float32)
    by_word = np.ascontiguousarray(scaled.reshape(k // 512, 128, 4, n).transpose(0, 1, 3, 2))
    if fmt == "e4m3":
        words = by_word.astype(ml_dtypes.float8_e4m3fn).view(np.uint8)
    else:
        c = by_word.astype(ml_dtypes.float4_e2m1fn).view(np.uint8) & 0xF
        words = (c[..., 0::2] | (c[..., 1::2] << 4)).reshape(k // 512, 128, 2 * n)
    return np.ascontiguousarray(words), np.ascontiguousarray(byte.astype(np.uint8).reshape(k // 512, 16, n))


def unpack_weight(words, scales, fmt):
    g, _, n = scales.shape
    words = np.ascontiguousarray(words).reshape(g, 128, n, -1)
    if fmt == "e4m3":
        vals = words.view(ml_dtypes.float8_e4m3fn).astype(np.float64)
    else:
        nib = np.empty((g, 128, n, 4), np.uint8)
        nib[..., 0::2] = words & 0xF
        nib[..., 1::2] = words >> 4
        vals = E2M1[nib]
    vals = vals * np.repeat(np.exp2(scales.astype(np.float64) - 127.0), 8, axis=1)[..., None]
    return vals.transpose(0, 1, 3, 2).reshape(g * 512, n)


def gelu(v):
    return 0.5 * v * (1.0 + np.tanh(np.sqrt(2.0 / np.pi) * (v + 0.044715 * v**3)))


K, H, T, S, T2, P = 512, 1024, 2048, 512, 1024, 512

def setup_inputs():
    n = np.random.standard_normal
    s = mx_kscale(K)[:, None]
    u = mx_kscale(H)[:, None]
    tab_words, tab_scales = pack_weight(n((K, T)) * s, "e4m3")
    w4_words, w4_scales = pack_weight(n((H, K)) / np.sqrt(H) / u / s.T, "e2m1")
    return {
        "tab_words": tab_words, "tab_scales": tab_scales,
        "offs": striped(np.random.permutation(T)[:S]),
        "offs2": striped(np.random.permutation(T2)[:S]),
        "offs3": striped(np.random.permutation(T2)[:P]),
        "offs4": striped(np.random.permutation(T2)[:P]),
        "wa": (n((K, H)) / np.sqrt(K) / s / u.T).astype(np.float32),
        "gin": (np.random.uniform(0.8, 1.6, H) * u[:, 0]).astype(np.float32),
        "gup": (np.random.uniform(1.0, 2.0, H) * u[:, 0]).astype(np.float32),
        "wgs": np.exp(0.3 * n((128, S))).astype(np.float32),
        "expected": (0.7 * n((H, T2)) * u).astype(np.float32),
        "w4_words": w4_words, "w4_scales": w4_scales,
        "gout": (np.random.uniform(0.5, 1.5, K) * s[:, 0]).astype(np.float32),
        "jobs": n((K, P)).astype(np.float32),
        "wgo": np.exp(0.3 * n((128, P))).astype(np.float32),
    }

def reference(tab_words, tab_scales, offs, offs2, offs3, offs4, wa, gin, gup, wgs,
              expected, w4_words, w4_scales, gout, jobs, wgo):
    v = unpack_weight(tab_words, tab_scales, "e4m3")[:, unstriped(offs)]
    pre = mxq(f64(wa), 0, "e4m3").T @ v
    h = f64(gup)[:, None] / (1.0 + np.exp(-f64(gin)[:, None] * pre))
    page = np.zeros((H, T2))
    page[:, unstriped(offs2)] = np.tile(f64(wgs), (H // 128, 1)) * h
    z = page - f64(expected)
    zq = mxq(z, 0, "e4m3")
    back = mxq(f64(wa).T, 0, "e4m3")
    w4 = unpack_weight(w4_words, w4_scales, "e2m1")
    y = back.T @ zq + w4.T @ zq
    x = y[:, unstriped(offs3)]
    x = f64(gout)[:, None] * x + f64(jobs)
    out = np.zeros((K, T2))
    out[:, unstriped(offs4)] = np.tile(f64(wgo), (K // 128, 1)) * x
    return out

@@ -1,0 +1,274 @@
+from contextlib import ExitStack
+
+import concourse.mybir as mybir
+from concourse.masks import make_identity
+
+K, H, T, S, T2, W = 512, 1024, 2048, 512, 1024, 512
+FLOPS = 2 * (K * H * S + 2 * H * K * T2)
+
+F32 = mybir.dt.float32
+BF16 = mybir.dt.bfloat16
+I32 = mybir.dt.int32
+U32 = mybir.dt.uint32
+U16 = mybir.dt.uint16
+U8 = mybir.dt.uint8
+FP8X4 = mybir.dt.float8_e4m3fn_x4
+FP4X4 = mybir.dt.float4_e2m1fn_x4
+MULT = mybir.AluOpType.mult
+ADD = mybir.AluOpType.add
+COPY = mybir.ActivationFunctionType.Copy
+SIGMOID = mybir.ActivationFunctionType.Sigmoid
+
+P = 128
+NPAGE = 3
+WA_PIECES = [(0, 1), (1, 2), (2, 4), (4, 8)]
+
+
+def tile_list_porter_dispatch_memory_kernel(tc, tab_words, tab_scales, offs, offs2, offs3, offs4, wa, gin, gup,
+                                                      wgs, expected, w4_words, w4_scales, gout, jobs, wgo, out):
+    nc = tc.nc
+    with ExitStack() as ctx:
+        keep = ctx.enter_context(tc.tile_pool(name="keep", bufs=1))
+        psum = ctx.enter_context(tc.psum_pool(name="psum", bufs=1))
+        bank = [psum.tile([P, 512], F32, name="bank%d" % i) for i in range(8)]
+
+        def sb(shape, dt, name, tag=None):
+            return keep.tile(shape, dt, name=name, tag=tag or name, align_bytes=64)
+
+        lists = [keep.tile([P, 32], U16, name="list%d" % i) for i in range(4)]
+        tabw = sb([P, T], U32, "tabw")
+        tabs = sb([P, T], U8, "tabs")
+        w4w = sb([P, 2, 2 * K], U8, "w4w")
+        w4s = sb([P, 2, K], U8, "w4s")
+        rows = sb([P, P], F32, "rows")
+        rows2 = sb([P, P], F32, "rows2")
+        cols2 = sb([P, 8], F32, "cols2")
+        clock = sb([P, 8], F32, "clock")
+        cols = sb([P, 32], F32, "cols")
+        ident = sb([P, P], F32, "ident")
+        warm = sb([P, 8], F32, "warm")
+        pages = [sb([P, T2], F32, "page%d" % i) for i in range(NPAGE)]
+        outs = [sb([P, T2], F32, "outp%d" % i) for i in range(2)]
+        wak = [sb([P, 4, P * (b - a)], F32, "wak%d" % a) for a, b in WA_PIECES]
+        wan = [sb([P, H], F32, "wan%d" % s) for s in range(4)]
+        exp_t = [sb([P, T2], F32, "exp%d" % s) for s in range(8)]
+        wgs_t = sb([P, S], F32, "wgs_t")
+        wgo_t = sb([P, W], F32, "wgo_t")
+        jobs_t = sb([P, 4, W], F32, "jobs_t")
+
+        nc.vector.memset(tabs[:].bitcast(I32), 0)
+        nc.vector.memset(rows[:], 0.0)
+        nc.vector.memset(w4s[:].rearrange("p a c -> p (a c)").bitcast(I32), 0)
+        nc.vector.memset(rows2[:], 0.0)
+        for pg in pages:
+            nc.vector.memset(pg[:], 0.0)
+        make_identity(nc, ident[:])
+        for o in outs:
+            nc.gpsimd.memset(o[:], 0.0)
+
+        wa_k = wa.rearrange("(p j) r -> p j r", j=4)
+
+        def load_wak(i):
+            a, b = WA_PIECES[i]
+            nc.sync.dma_start(out=wak[i][:], in_=wa_k[:, :, P * a:P * b])
+
+        nc.sync.dma_start(lists[0][:], offs)
+        load_wak(0)
+        nc.sync.dma_start(out=tabw[:].bitcast(I32), in_=tab_words[0].rearrange("p t i -> p (t i)").bitcast(I32))
+        for q in range(4):
+            nc.sync.dma_start(out=tabs[32 * q:32 * q + 4, :].bitcast(I32), in_=tab_scales[0, 4 * q:4 * q + 4, :].bitcast(I32))
+        nc.sync.dma_start(out=rows[0:8, :], in_=gin.rearrange("(s p) -> s p", p=P))
+        nc.sync.dma_start(out=rows[8:16, :], in_=gup.rearrange("(s p) -> s p", p=P))
+        nc.sync.dma_start(out=wgs_t[:], in_=wgs)
+        nc.sync.dma_start(lists[1][:], offs2)
+        load_wak(1)
+        load_wak(2)
+        load_wak(3)
+
+        def load_exp(s):
+            nc.sync.dma_start(out=exp_t[s][:], in_=expected[P * s:P * (s + 1), :])
+
+        def load_wan(s):
+            nc.sync.dma_start(out=wan[s][:], in_=wa[P * s:P * (s + 1), :])
+
+        load_exp(0)
+        load_exp(1)
+        load_wan(0)
+        load_exp(2)
+        load_wan(1)
+        load_exp(3)
+        load_exp(4)
+        nc.sync.dma_start(out=w4w[:].bitcast(I32), in_=w4_words.rearrange("a p c -> p a c").bitcast(I32))
+        for q in range(4):
+            nc.sync.dma_start(out=w4s[32 * q:32 * q + 4, :, :].bitcast(I32),
+                              in_=w4_scales[:, 4 * q:4 * q + 4, :].rearrange("a r c -> r a c").bitcast(I32))
+        nc.sync.dma_start(out=rows2[0:4, :], in_=gout.rearrange("(s p) -> s p", p=P))
+        load_exp(5)
+        load_wan(2)
+        load_exp(6)
+        load_wan(3)
+        load_exp(7)
+        nc.sync.dma_start(lists[2][:], offs3)
+        nc.sync.dma_start(lists[3][:], offs4)
+        nc.sync.dma_start(out=jobs_t[:], in_=jobs.rearrange("(s p) m -> p s m", p=P))
+        nc.sync.dma_start(out=wgo_t[:], in_=wgo)
+
+        nc.scalar.activation(warm[:, 0:1], ident[:, 0:1], SIGMOID)
+        nc.tensor.transpose(bank[5][:, 0:P], rows[:], ident[:])
+        nc.scalar.copy(cols[:, 0:16], bank[5][:, 0:16])
+
+        vw = sb([P, S], U32, "vw")
+        vs = sb([P, S], U8, "vs")
+
+        def fetch(h):
+            nc.vector.tensor_copy(vw[:, 256 * h:256 * (h + 1)], tabw[:].indirect(lists[0][:, 16 * h:16 * (h + 1)]))
+            nc.vector.tensor_copy(vs[:, 256 * h:256 * (h + 1)], tabs[:].indirect(lists[0][:, 16 * h:16 * (h + 1)]))
+
+        wac = [sb([P, P * (b - a)], U32, "wac%d" % a) for a, b in WA_PIECES]
+        was = [sb([P, P * (b - a)], U8, "was%d" % a) for a, b in WA_PIECES]
+        hs = [None] + [sb([P, S], F32, "h%d" % s) for s in range(1, 8)]
+
+        def quant_wak(i):
+            a, b = WA_PIECES[i]
+            g = sb([P, 4 * P * (b - a)], BF16, "wag%d" % i)
+            nc.scalar.copy(g[:].rearrange("p (c i j) -> p c j i", i=4, j=4), wak[i][:].rearrange("p j (c i) -> p c j i", i=4))
+            nc.vector.quantize_mx(out=wac[i][:].bitcast(FP8X4), scales=was[i][:], in_=g[:])
+
+        def encode(i):
+            a, b = WA_PIECES[i]
+            for s in range(a, b):
+                c = slice(P * (s - a), P * (s - a + 1))
+                acc = bank[7 - s % 2]
+                nc.tensor.matmul_mx(out=acc[:], lhsT=wac[i][:, c].bitcast(FP8X4), lhsT_scale=was[i][:, c],
+                                    rhs=vw[:].bitcast(FP8X4), rhs_scale=vs[:], start=True, stop=True)
+                nc.scalar.activation(hs[s][:], acc[:], SIGMOID, scale=cols[:, s:s + 1])
+
+        quant_wak(0)
+        fetch(0)
+        h0 = [sb([P, 256], F32, "h0%d" % h) for h in range(2)]
+        for h in range(2):
+            if h == 1:
+                fetch(1)
+            c = slice(256 * h, 256 * (h + 1))
+            nc.tensor.matmul_mx(out=bank[6 + h][:, 0:256], lhsT=wac[0][:].bitcast(FP8X4), lhsT_scale=was[0][:],
+                                rhs=vw[:, c].bitcast(FP8X4), rhs_scale=vs[:, c], start=True, stop=True)
+            nc.scalar.activation(h0[h][:], bank[6 + h][:, 0:256], SIGMOID, scale=cols[:, 0:1])
+            if h == 0:
+                nc.gpsimd.tensor_copy(clock[:, 1:2], h0[0][:, 0:1])
+        for i in range(1, 4):
+            quant_wak(i)
+            encode(i)
+
+        zt = [[sb([P, 2048], BF16, "zt%d%d" % (b, h)) for h in range(2)] for b in range(2)]
+        zc = [[sb([P, 512], U32, "zc%d%d" % (b, h)) for h in range(2)] for b in range(2)]
+        zs = [[sb([P, 512], U8, "zs%d%d" % (b, h)) for h in range(2)] for b in range(2)]
+        wtc = [sb([P, 256], U32, "wtc%d" % s) for s in range(4)]
+        wts = [sb([P, 256], U8, "wts%d" % s) for s in range(4)]
+        pre_tag = {1: "wag2", 2: "wag3", 5: "wtin0", 6: "wtin1", 7: "zin0"}
+
+        def place(s):
+            pre = sb([P, S], F32, "pre%d" % s, pre_tag.get(s))
+            nc.vector.tensor_scalar(pre[:], wgs_t[:], cols[:, 8 + s:9 + s], -1.0, MULT, MULT)
+            pg = pages[s % NPAGE]
+            if s == 0:
+                for h in range(2):
+                    nc.vector.tensor_tensor(pg[:].indirect(lists[1][:, 16 * h:16 * (h + 1)]), h0[h][:], pre[:, 256 * h:256 * (h + 1)], MULT)
+            else:
+                nc.vector.tensor_tensor(pg[:].indirect(lists[1][:]), hs[s][:], pre[:], MULT)
+
+        def level1(s, last=False):
+            pg = pages[s % NPAGE]
+            b, sl = divmod(s, 4)
+            for h in range(2):
+                acc = bank[2 * (s % 2) + h]
+                for tb in range(4):
+                    c = slice(512 * h + P * tb, 512 * h + P * (tb + 1))
+                    nc.tensor.matmul(acc[:, P * tb:P * (tb + 1)], exp_t[s][:, c], ident[:], start=(tb == 0), stop=False, is_transpose=True)
+            for h in range(2):
+                acc = bank[2 * (s % 2) + h]
+                for tb in range(4):
+                    c = slice(512 * h + P * tb, 512 * h + P * (tb + 1))
+                    nc.tensor.matmul(acc[:, P * tb:P * (tb + 1)], pg[:, c], ident[:], start=False, stop=(tb == 3), is_transpose=True)
+                dst = zt[b][h][:].rearrange("c (u t q e) -> c u t q e", u=2, t=4, e=2)[:, :, :, 32 * sl:32 * sl + 32, :]
+                src = acc[:].rearrange("c (t q u e) -> c u t q e", t=4, u=2, e=2)
+                if last and h == 1:
+                    nc.vector.tensor_scalar(dst, src, -1.0, None, MULT)
+                else:
+                    nc.scalar.activation(dst, src, COPY, scale=-1.0)
+
+        def level2(b, banks, on_vector):
+            zin = sb([P, 4096], BF16, "zin%d" % b)
+            zw = zin[:].bitcast(F32)
+            for h in range(2):
+                words = zt[b][h][:].bitcast(F32)
+                for g in range(2):
+                    qd = 2 * h + g
+                    acc = bank[banks[qd]]
+                    for u in range(2):
+                        for t in range(2):
+                            o = 512 * u + P * (2 * g + t)
+                            nc.tensor.transpose(acc[:, 256 * u + P * t:256 * u + P * (t + 1)], words[:, o:o + P], ident[:])
+                    dst = zw[:, 512 * qd:512 * (qd + 1)].rearrange("p (c u) -> p c u", u=2)
+                    src = acc[:].rearrange("p (u c) -> p c u", u=2)
+                    if qd in on_vector:
+                        nc.vector.tensor_copy(dst, src)
+                    else:
+                        nc.scalar.copy(dst, src)
+                nc.vector.quantize_mx(out=zc[b][h][:].bitcast(FP8X4), scales=zs[b][h][:], in_=zin[:, 2048 * h:2048 * (h + 1)])
+
+        def back_weights(s):
+            wb = sb([P, H], BF16, "wb%d" % s)
+            nc.scalar.copy(wb[:].rearrange("n (u q e) -> n u q e", u=2, e=2), wan[s][:].rearrange("n (q u e) -> n u q e", u=2, e=2))
+            words = wb[:].bitcast(F32)
+            acc = bank[4 + s % 2]
+            for b in range(2):
+                for u in range(2):
+                    o = 256 * u + P * b
+                    nc.tensor.transpose(acc[:, 256 * b + P * u:256 * b + P * (u + 1)], words[:, o:o + P], ident[:])
+            wtin = sb([P, H], BF16, "wtin%d" % s)
+            nc.scalar.copy(wtin[:].bitcast(F32).rearrange("p (b n u) -> p b n u", b=2, u=2),
+                           acc[:].rearrange("p (b u n) -> p b n u", b=2, u=2))
+            nc.vector.quantize_mx(out=wtc[s][:].bitcast(FP8X4), scales=wts[s][:], in_=wtin[:])
+
+        ybank = [(6, 7), (2, 3), (4, 5), (0, 1)]
+
+        def project(s, b, h):
+            acc = bank[ybank[s][h]]
+            c = slice(P * b, P * (b + 1))
+            nc.tensor.matmul_mx(out=acc[:], lhsT=wtc[s][:, c].bitcast(FP8X4), lhsT_scale=wts[s][:, c],
+                                rhs=zc[b][h][:].bitcast(FP8X4), rhs_scale=zs[b][h][:], start=(b == 0), stop=False)
+            nc.tensor.matmul_mx(out=acc[:], lhsT=w4w[:, b, 256 * s:256 * (s + 1)].bitcast(FP4X4), lhsT_scale=w4s[:, b, P * s:P * (s + 1)],
+                                rhs=zc[b][h][:].bitcast(FP8X4), rhs_scale=zs[b][h][:], start=False, stop=(b == 1))
+
+        for s in range(4):
+            place(s)
+            level1(s)
+            if s >= 2:
+                back_weights(s - 2)
+        level2(0, [4, 5, 4, 5], [])
+        for s in range(4, 7):
+            place(s)
+            level1(s)
+            if s <= 5:
+                back_weights(s - 2)
+        nc.tensor.transpose(bank[4][:, 0:P], rows2[:], ident[:])
+        nc.scalar.copy(cols2[:, 0:4], bank[4][:, 0:4])
+        place(7)
+        nc.gpsimd.tensor_copy(clock[:, 0:1], pages[7 % NPAGE][:, 0:1])
+        project(0, 0, 0)
+        project(0, 0, 1)
+        level1(7, last=True)
+        level2(1, [4, 5, 0, 1], [1])
+
+        for s in range(4):
+            y = sb([P, T2], F32, "y%d" % s, "exp%d" % s)
+            for h in range(2):
+                if s > 0:
+                    project(s, 0, h)
+                project(s, 1, h)
+                nc.scalar.activation(y[:, 512 * h:512 * (h + 1)], bank[ybank[s][h]][:], COPY, scale=cols2[:, s:s + 1])
+            x = sb([P, W], F32, "x%d" % s, "h%d" % (s + 1))
+            nc.vector.tensor_tensor(x[:], y[:].indirect(lists[2][:]), jobs_t[:, s, :], ADD)
+            o = outs[s % 2]
+            nc.vector.tensor_tensor(o[:].indirect(lists[3][:]), x[:], wgo_t[:], MULT)
+            nc.sync.dma_start(out=out[P * s:P * (s + 1), :], in_=o[:])

@@ -21,7 +21,7 @@ SIGMOID = mybir.ActivationFunctionType.Sigmoid
 
 P = 128
 NPAGE = 3
-WA_PIECES = [(0, 1), (1, 2), (2, 4), (4, 8)]
+WA_PIECES = [(0, 2), (2, 4), (4, 8)]
 
 
 def tile_list_porter_dispatch_memory_kernel(tc, tab_words, tab_scales, offs, offs2, offs3, offs4, wa, gin, gup,
@@ -43,7 +43,6 @@ def tile_list_porter_dispatch_memory_kernel(tc, tab_words, tab_scales, offs, off
         rows = sb([P, P], F32, "rows")
         rows2 = sb([P, P], F32, "rows2")
         cols2 = sb([P, 8], F32, "cols2")
-        clock = sb([P, 8], F32, "clock")
         cols = sb([P, 32], F32, "cols")
         ident = sb([P, P], F32, "ident")
         warm = sb([P, 8], F32, "warm")
@@ -56,15 +55,15 @@ def tile_list_porter_dispatch_memory_kernel(tc, tab_words, tab_scales, offs, off
         wgo_t = sb([P, W], F32, "wgo_t")
         jobs_t = sb([P, 4, W], F32, "jobs_t")
 
+        nc.gpsimd.memset(rows[:], 0.0)
         nc.vector.memset(tabs[:].bitcast(I32), 0)
-        nc.vector.memset(rows[:], 0.0)
         nc.vector.memset(w4s[:].rearrange("p a c -> p (a c)").bitcast(I32), 0)
         nc.vector.memset(rows2[:], 0.0)
         for pg in pages:
             nc.vector.memset(pg[:], 0.0)
         make_identity(nc, ident[:])
         for o in outs:
-            nc.gpsimd.memset(o[:], 0.0)
+            nc.vector.memset(o[:], 0.0)
 
         wa_k = wa.rearrange("(p j) r -> p j r", j=4)
 
@@ -74,16 +73,15 @@ def tile_list_porter_dispatch_memory_kernel(tc, tab_words, tab_scales, offs, off
 
         nc.sync.dma_start(lists[0][:], offs)
         load_wak(0)
-        nc.sync.dma_start(out=tabw[:].bitcast(I32), in_=tab_words[0].rearrange("p t i -> p (t i)").bitcast(I32))
-        for q in range(4):
-            nc.sync.dma_start(out=tabs[32 * q:32 * q + 4, :].bitcast(I32), in_=tab_scales[0, 4 * q:4 * q + 4, :].bitcast(I32))
         nc.sync.dma_start(out=rows[0:8, :], in_=gin.rearrange("(s p) -> s p", p=P))
         nc.sync.dma_start(out=rows[8:16, :], in_=gup.rearrange("(s p) -> s p", p=P))
+        for q in range(4):
+            nc.sync.dma_start(out=tabs[32 * q:32 * q + 4, :].bitcast(I32), in_=tab_scales[0, 4 * q:4 * q + 4, :].bitcast(I32))
+        nc.sync.dma_start(out=tabw[:].bitcast(I32), in_=tab_words[0].rearrange("p t i -> p (t i)").bitcast(I32))
         nc.sync.dma_start(out=wgs_t[:], in_=wgs)
         nc.sync.dma_start(lists[1][:], offs2)
         load_wak(1)
         load_wak(2)
-        load_wak(3)
 
         def load_exp(s):
             nc.sync.dma_start(out=exp_t[s][:], in_=expected[P * s:P * (s + 1), :])
@@ -122,7 +120,6 @@ def tile_list_porter_dispatch_memory_kernel(tc, tab_words, tab_scales, offs, off
 
         def fetch(h):
             nc.vector.tensor_copy(vw[:, 256 * h:256 * (h + 1)], tabw[:].indirect(lists[0][:, 16 * h:16 * (h + 1)]))
-            nc.vector.tensor_copy(vs[:, 256 * h:256 * (h + 1)], tabs[:].indirect(lists[0][:, 16 * h:16 * (h + 1)]))
 
         wac = [sb([P, P * (b - a)], U32, "wac%d" % a) for a, b in WA_PIECES]
         was = [sb([P, P * (b - a)], U8, "was%d" % a) for a, b in WA_PIECES]
@@ -130,19 +127,20 @@ def tile_list_porter_dispatch_memory_kernel(tc, tab_words, tab_scales, offs, off
 
         def quant_wak(i):
             a, b = WA_PIECES[i]
-            g = sb([P, 4 * P * (b - a)], BF16, "wag%d" % i)
+            g = sb([P, 4 * P * (b - a)], BF16, "wag%d" % i, ["wag0", "h00", "h01"][i])
             nc.scalar.copy(g[:].rearrange("p (c i j) -> p c j i", i=4, j=4), wak[i][:].rearrange("p j (c i) -> p c j i", i=4))
             nc.vector.quantize_mx(out=wac[i][:].bitcast(FP8X4), scales=was[i][:], in_=g[:])
 
         def encode(i):
             a, b = WA_PIECES[i]
-            for s in range(a, b):
+            for s in range(max(a, 1), b):
                 c = slice(P * (s - a), P * (s - a + 1))
-                acc = bank[7 - s % 2]
+                acc = bank[2 if s == 1 else 6 + s % 2]
                 nc.tensor.matmul_mx(out=acc[:], lhsT=wac[i][:, c].bitcast(FP8X4), lhsT_scale=was[i][:, c],
                                     rhs=vw[:].bitcast(FP8X4), rhs_scale=vs[:], start=True, stop=True)
                 nc.scalar.activation(hs[s][:], acc[:], SIGMOID, scale=cols[:, s:s + 1])
 
+        nc.vector.tensor_copy(vs[:], tabs[:].indirect(lists[0][:]))
         quant_wak(0)
         fetch(0)
         h0 = [sb([P, 256], F32, "h0%d" % h) for h in range(2)]
@@ -150,24 +148,22 @@ def tile_list_porter_dispatch_memory_kernel(tc, tab_words, tab_scales, offs, off
             if h == 1:
                 fetch(1)
             c = slice(256 * h, 256 * (h + 1))
-            nc.tensor.matmul_mx(out=bank[6 + h][:, 0:256], lhsT=wac[0][:].bitcast(FP8X4), lhsT_scale=was[0][:],
+            nc.tensor.matmul_mx(out=bank[h][:, 0:256], lhsT=wac[0][:, 0:P].bitcast(FP8X4), lhsT_scale=was[0][:, 0:P],
                                 rhs=vw[:, c].bitcast(FP8X4), rhs_scale=vs[:, c], start=True, stop=True)
-            nc.scalar.activation(h0[h][:], bank[6 + h][:, 0:256], SIGMOID, scale=cols[:, 0:1])
-            if h == 0:
-                nc.gpsimd.tensor_copy(clock[:, 1:2], h0[0][:, 0:1])
-        for i in range(1, 4):
-            quant_wak(i)
-            encode(i)
+            nc.scalar.activation(h0[h][:], bank[h][:, 0:256], SIGMOID, scale=cols[:, 0:1])
+        encode(0)
 
         zt = [[sb([P, 2048], BF16, "zt%d%d" % (b, h)) for h in range(2)] for b in range(2)]
         zc = [[sb([P, 512], U32, "zc%d%d" % (b, h)) for h in range(2)] for b in range(2)]
         zs = [[sb([P, 512], U8, "zs%d%d" % (b, h)) for h in range(2)] for b in range(2)]
         wtc = [sb([P, 256], U32, "wtc%d" % s) for s in range(4)]
         wts = [sb([P, 256], U8, "wts%d" % s) for s in range(4)]
-        pre_tag = {1: "wag2", 2: "wag3", 5: "wtin0", 6: "wtin1", 7: "zin0"}
+        pre_tag = {1: "h00", 2: "h01", 5: "wtin0", 6: "wtin1", 7: "zin0"}
+
+        early = sb([P, 3, S], F32, "early", "tabw")
 
         def place(s):
-            pre = sb([P, S], F32, "pre%d" % s, pre_tag.get(s))
+            pre = early[:, (0, 3, 4).index(s), :] if s in (0, 3, 4) else sb([P, S], F32, "pre%d" % s, pre_tag[s])
             nc.vector.tensor_scalar(pre[:], wgs_t[:], cols[:, 8 + s:9 + s], -1.0, MULT, MULT)
             pg = pages[s % NPAGE]
             if s == 0:
@@ -214,10 +210,14 @@ def tile_list_porter_dispatch_memory_kernel(tc, tab_words, tab_scales, offs, off
                         nc.vector.tensor_copy(dst, src)
                     else:
                         nc.scalar.copy(dst, src)
-                nc.vector.quantize_mx(out=zc[b][h][:].bitcast(FP8X4), scales=zs[b][h][:], in_=zin[:, 2048 * h:2048 * (h + 1)])
+                    if b == 1:
+                        c = slice(256 * g, 256 * (g + 1))
+                        nc.vector.quantize_mx(out=zc[b][h][:, c].bitcast(FP8X4), scales=zs[b][h][:, c], in_=zin[:, 1024 * qd:1024 * (qd + 1)])
+                if b == 0:
+                    nc.vector.quantize_mx(out=zc[b][h][:].bitcast(FP8X4), scales=zs[b][h][:], in_=zin[:, 2048 * h:2048 * (h + 1)])
 
         def back_weights(s):
-            wb = sb([P, H], BF16, "wb%d" % s)
+            wb = sb([P, H], BF16, "wb%d" % s, "h%d" % (1, 2, 5, 6)[s])
             nc.scalar.copy(wb[:].rearrange("n (u q e) -> n u q e", u=2, e=2), wan[s][:].rearrange("n (q u e) -> n u q e", u=2, e=2))
             words = wb[:].bitcast(F32)
             acc = bank[4 + s % 2]
@@ -242,6 +242,10 @@ def tile_list_porter_dispatch_memory_kernel(tc, tab_words, tab_scales, offs, off
 
         for s in range(4):
             place(s)
+            if s == 0:
+                for i in (1, 2):
+                    quant_wak(i)
+                    encode(i)
             level1(s)
             if s >= 2:
                 back_weights(s - 2)
@@ -249,12 +253,11 @@ def tile_list_porter_dispatch_memory_kernel(tc, tab_words, tab_scales, offs, off
         for s in range(4, 7):
             place(s)
             level1(s)
-            if s <= 5:
-                back_weights(s - 2)
+            if s >= 5:
+                back_weights(s - 3)
         nc.tensor.transpose(bank[4][:, 0:P], rows2[:], ident[:])
         nc.scalar.copy(cols2[:, 0:4], bank[4][:, 0:4])
         place(7)
-        nc.gpsimd.tensor_copy(clock[:, 0:1], pages[7 % NPAGE][:, 0:1])
         project(0, 0, 0)
         project(0, 0, 1)
         level1(7, last=True)

@@ -3,7 +3,7 @@ from contextlib import ExitStack
 import concourse.mybir as mybir
 from concourse.masks import make_identity
 
-K, H, T, S, T2, W = 512, 1024, 2048, 512, 1024, 512
+K, H, T, S, T2, WATCHED = 512, 1024, 2048, 512, 1024, 512
 FLOPS = 2 * (K * H * S + 2 * H * K * T2)
 
 F32 = mybir.dt.float32
@@ -20,8 +20,14 @@ COPY = mybir.ActivationFunctionType.Copy
 SIGMOID = mybir.ActivationFunctionType.Sigmoid
 
 P = 128
-NPAGE = 3
+BANK = 512
+HALF_LIST = 256
+QUARTER = 256
+SLICES, NTILES = H // P, K // P
+LAST = SLICES - 1
+PAGES = 3
 WA_PIECES = [(0, 2), (2, 4), (4, 8)]
+Y_BANKS = [(6, 7), (0, 1), (4, 5), (2, 3)]
 
 
 def tile_list_porter_dispatch_memory_kernel(tc, tab_words, tab_scales, offs, offs2, offs3, offs4, wa, gin, gup,
@@ -30,248 +36,259 @@ def tile_list_porter_dispatch_memory_kernel(tc, tab_words, tab_scales, offs, off
     with ExitStack() as ctx:
         keep = ctx.enter_context(tc.tile_pool(name="keep", bufs=1))
         psum = ctx.enter_context(tc.psum_pool(name="psum", bufs=1))
-        bank = [psum.tile([P, 512], F32, name="bank%d" % i) for i in range(8)]
+        bank = [psum.tile([P, BANK], F32, name="bank%d" % i) for i in range(8)]
 
         def sb(shape, dt, name, tag=None):
             return keep.tile(shape, dt, name=name, tag=tag or name, align_bytes=64)
 
-        lists = [keep.tile([P, 32], U16, name="list%d" % i) for i in range(4)]
-        tabw = sb([P, T], U32, "tabw")
-        tabs = sb([P, T], U8, "tabs")
-        w4w = sb([P, 2, 2 * K], U8, "w4w")
-        w4s = sb([P, 2, K], U8, "w4s")
-        rows = sb([P, P], F32, "rows")
-        rows2 = sb([P, P], F32, "rows2")
-        cols2 = sb([P, 8], F32, "cols2")
-        cols = sb([P, 32], F32, "cols")
+        lists = [keep.tile([P, S // 16], U16, name="list%d" % i) for i in range(4)]
+        tab_w = sb([P, T], U32, "tab_w")
+        tab_s = sb([P, T], U8, "tab_s")
+        w4_w = sb([P, 2, 2 * K], U8, "w4_w")
+        w4_s = sb([P, 2, K], U8, "w4_s")
+        gain_rows = sb([P, P], F32, "gain_rows")
+        gout_rows = sb([P, P], F32, "gout_rows")
+        gout_cols = sb([P, 8], F32, "gout_cols")
+        gain_cols = sb([P, 32], F32, "gain_cols")
         ident = sb([P, P], F32, "ident")
         warm = sb([P, 8], F32, "warm")
-        pages = [sb([P, T2], F32, "page%d" % i) for i in range(NPAGE)]
-        outs = [sb([P, T2], F32, "outp%d" % i) for i in range(2)]
-        wak = [sb([P, 4, P * (b - a)], F32, "wak%d" % a) for a, b in WA_PIECES]
-        wan = [sb([P, H], F32, "wan%d" % s) for s in range(4)]
-        exp_t = [sb([P, T2], F32, "exp%d" % s) for s in range(8)]
+        pages = [sb([P, T2], F32, "page%d" % i) for i in range(PAGES)]
+        handsets = [sb([P, T2], F32, "handset%d" % i) for i in range(2)]
+        wa_by_k = [sb([P, 4, P * (b - a)], F32, "wa_by_k%d" % i) for i, (a, b) in enumerate(WA_PIECES)]
+        wa_by_n = [sb([P, H], F32, "wa_by_n%d" % s) for s in range(NTILES)]
+        exp_t = [sb([P, T2], F32, "exp%d" % s) for s in range(SLICES)]
         wgs_t = sb([P, S], F32, "wgs_t")
-        wgo_t = sb([P, W], F32, "wgo_t")
-        jobs_t = sb([P, 4, W], F32, "jobs_t")
+        wgo_t = sb([P, WATCHED], F32, "wgo_t")
+        jobs_t = sb([P, NTILES, WATCHED], F32, "jobs_t")
 
-        nc.gpsimd.memset(rows[:], 0.0)
-        nc.vector.memset(tabs[:].bitcast(I32), 0)
-        nc.vector.memset(w4s[:].rearrange("p a c -> p (a c)").bitcast(I32), 0)
-        nc.vector.memset(rows2[:], 0.0)
-        for pg in pages:
-            nc.vector.memset(pg[:], 0.0)
-        make_identity(nc, ident[:])
-        for o in outs:
-            nc.vector.memset(o[:], 0.0)
+        nc.gpsimd.memset(ident[:], 0.0)
+        nc.gpsimd.memset(gain_rows[:], 0.0)
+        make_identity(nc, ident[:], nomemset=True)
+        nc.vector.memset(tab_s[:].bitcast(I32), 0)
+        nc.vector.memset(pages[0][:], 0.0)
+        nc.vector.memset(w4_s[:].rearrange("p a c -> p (a c)").bitcast(I32), 0)
+        nc.vector.memset(gout_rows[:], 0.0)
+        nc.vector.memset(pages[1][:], 0.0)
+        nc.vector.memset(handsets[0][:], 0.0)
+        nc.gpsimd.memset(pages[2][:], 0.0)
+        nc.gpsimd.memset(handsets[1][:], 0.0)
 
         wa_k = wa.rearrange("(p j) r -> p j r", j=4)
 
-        def load_wak(i):
+        def load_wa_by_k(i):
             a, b = WA_PIECES[i]
-            nc.sync.dma_start(out=wak[i][:], in_=wa_k[:, :, P * a:P * b])
+            nc.sync.dma_start(out=wa_by_k[i][:], in_=wa_k[:, :, P * a:P * b])
 
-        nc.sync.dma_start(lists[0][:], offs)
-        load_wak(0)
-        nc.sync.dma_start(out=rows[0:8, :], in_=gin.rearrange("(s p) -> s p", p=P))
-        nc.sync.dma_start(out=rows[8:16, :], in_=gup.rearrange("(s p) -> s p", p=P))
-        for q in range(4):
-            nc.sync.dma_start(out=tabs[32 * q:32 * q + 4, :].bitcast(I32), in_=tab_scales[0, 4 * q:4 * q + 4, :].bitcast(I32))
-        nc.sync.dma_start(out=tabw[:].bitcast(I32), in_=tab_words[0].rearrange("p t i -> p (t i)").bitcast(I32))
-        nc.sync.dma_start(out=wgs_t[:], in_=wgs)
-        nc.sync.dma_start(lists[1][:], offs2)
-        load_wak(1)
-        load_wak(2)
-
-        def load_exp(s):
+        def load_expected(s):
             nc.sync.dma_start(out=exp_t[s][:], in_=expected[P * s:P * (s + 1), :])
 
-        def load_wan(s):
-            nc.sync.dma_start(out=wan[s][:], in_=wa[P * s:P * (s + 1), :])
+        def load_wa_by_n(s):
+            nc.sync.dma_start(out=wa_by_n[s][:], in_=wa[P * s:P * (s + 1), :])
 
-        load_exp(0)
-        load_exp(1)
-        load_wan(0)
-        load_exp(2)
-        load_wan(1)
-        load_exp(3)
-        load_exp(4)
-        nc.sync.dma_start(out=w4w[:].bitcast(I32), in_=w4_words.rearrange("a p c -> p a c").bitcast(I32))
+        nc.sync.dma_start(lists[0][:], offs)
+        load_wa_by_k(0)
+        nc.sync.dma_start(out=gain_rows[0:8, :], in_=gin.rearrange("(s p) -> s p", p=P))
+        nc.sync.dma_start(out=gain_rows[8:16, :], in_=gup.rearrange("(s p) -> s p", p=P))
         for q in range(4):
-            nc.sync.dma_start(out=w4s[32 * q:32 * q + 4, :, :].bitcast(I32),
+            nc.sync.dma_start(out=tab_s[32 * q:32 * q + 4, :].bitcast(I32), in_=tab_scales[0, 4 * q:4 * q + 4, :].bitcast(I32))
+        nc.sync.dma_start(out=tab_w[:].bitcast(I32), in_=tab_words[0].rearrange("p t i -> p (t i)").bitcast(I32))
+        nc.sync.dma_start(out=wgs_t[:], in_=wgs)
+        nc.sync.dma_start(lists[1][:], offs2)
+        load_wa_by_k(1)
+        load_wa_by_k(2)
+        load_expected(0)
+        load_expected(1)
+        load_wa_by_n(0)
+        load_expected(2)
+        load_wa_by_n(1)
+        load_expected(3)
+        load_expected(4)
+        nc.sync.dma_start(out=w4_w[:].bitcast(I32), in_=w4_words.rearrange("a p c -> p a c").bitcast(I32))
+        for q in range(4):
+            nc.sync.dma_start(out=w4_s[32 * q:32 * q + 4, :, :].bitcast(I32),
                               in_=w4_scales[:, 4 * q:4 * q + 4, :].rearrange("a r c -> r a c").bitcast(I32))
-        nc.sync.dma_start(out=rows2[0:4, :], in_=gout.rearrange("(s p) -> s p", p=P))
-        load_exp(5)
-        load_wan(2)
-        load_exp(6)
-        load_wan(3)
-        load_exp(7)
+        nc.sync.dma_start(out=gout_rows[0:4, :], in_=gout.rearrange("(s p) -> s p", p=P))
+        load_expected(5)
+        load_wa_by_n(2)
+        load_expected(6)
+        load_wa_by_n(3)
+        load_expected(7)
         nc.sync.dma_start(lists[2][:], offs3)
         nc.sync.dma_start(lists[3][:], offs4)
         nc.sync.dma_start(out=jobs_t[:], in_=jobs.rearrange("(s p) m -> p s m", p=P))
         nc.sync.dma_start(out=wgo_t[:], in_=wgo)
 
         nc.scalar.activation(warm[:, 0:1], ident[:, 0:1], SIGMOID)
-        nc.tensor.transpose(bank[5][:, 0:P], rows[:], ident[:])
-        nc.scalar.copy(cols[:, 0:16], bank[5][:, 0:16])
 
-        vw = sb([P, S], U32, "vw")
-        vs = sb([P, S], U8, "vs")
+        nc.tensor.transpose(bank[0][:, 0:P], gain_rows[:], ident[:])
+        gin_first = sb([P, 2], F32, "gin_first")
+        nc.scalar.copy(gin_first[:], bank[0][:, 0:2])
+        nc.scalar.activation(gain_cols[:, 8:16], bank[0][:, 8:16], COPY, scale=-1.0)
+        nc.scalar.copy(gain_cols[:, 2:8], bank[0][:, 2:8])
 
-        def fetch(h):
-            nc.vector.tensor_copy(vw[:, 256 * h:256 * (h + 1)], tabw[:].indirect(lists[0][:, 16 * h:16 * (h + 1)]))
+        v_w = sb([P, S], U32, "v_w")
+        v_s = sb([P, S], U8, "v_s")
+        wa_w = [sb([P, P * (b - a)], U32, "wa_w%d" % i) for i, (a, b) in enumerate(WA_PIECES)]
+        wa_s = [sb([P, P * (b - a)], U8, "wa_s%d" % i) for i, (a, b) in enumerate(WA_PIECES)]
+        sig = {s: sb([P, S], F32, "sig%d" % s) for s in range(1, SLICES)}
 
-        wac = [sb([P, P * (b - a)], U32, "wac%d" % a) for a, b in WA_PIECES]
-        was = [sb([P, P * (b - a)], U8, "was%d" % a) for a, b in WA_PIECES]
-        hs = [None] + [sb([P, S], F32, "h%d" % s) for s in range(1, 8)]
-
-        def quant_wak(i):
+        def quantise_wa(i):
             a, b = WA_PIECES[i]
-            g = sb([P, 4 * P * (b - a)], BF16, "wag%d" % i, ["wag0", "h00", "h01"][i])
-            nc.scalar.copy(g[:].rearrange("p (c i j) -> p c j i", i=4, j=4), wak[i][:].rearrange("p j (c i) -> p c j i", i=4))
-            nc.vector.quantize_mx(out=wac[i][:].bitcast(FP8X4), scales=was[i][:], in_=g[:])
+            grouped = sb([P, 4 * P * (b - a)], BF16, "wa_grouped%d" % i, (None, "gin_first", "sig0_0")[i])
+            nc.scalar.copy(grouped[:].rearrange("p (c i j) -> p c j i", i=4, j=4),
+                           wa_by_k[i][:].rearrange("p j (c i) -> p c j i", i=4))
+            nc.vector.quantize_mx(out=wa_w[i][:].bitcast(FP8X4), scales=wa_s[i][:], in_=grouped[:])
 
         def encode(i):
             a, b = WA_PIECES[i]
             for s in range(max(a, 1), b):
                 c = slice(P * (s - a), P * (s - a + 1))
                 acc = bank[2 if s == 1 else 6 + s % 2]
-                nc.tensor.matmul_mx(out=acc[:], lhsT=wac[i][:, c].bitcast(FP8X4), lhsT_scale=was[i][:, c],
-                                    rhs=vw[:].bitcast(FP8X4), rhs_scale=vs[:], start=True, stop=True)
-                nc.scalar.activation(hs[s][:], acc[:], SIGMOID, scale=cols[:, s:s + 1])
+                nc.tensor.matmul_mx(out=acc[:], lhsT=wa_w[i][:, c].bitcast(FP8X4), lhsT_scale=wa_s[i][:, c],
+                                    rhs=v_w[:].bitcast(FP8X4), rhs_scale=v_s[:], start=True, stop=True)
+                nc.scalar.activation(sig[s][:], acc[:], SIGMOID, scale=(gin_first if s == 1 else gain_cols)[:, s:s + 1])
 
-        nc.vector.tensor_copy(vs[:], tabs[:].indirect(lists[0][:]))
-        quant_wak(0)
-        fetch(0)
-        h0 = [sb([P, 256], F32, "h0%d" % h) for h in range(2)]
+        nc.vector.tensor_copy(v_s[:], tab_s[:].indirect(lists[0][:]))
+        quantise_wa(0)
+        sig0 = [sb([P, HALF_LIST], F32, "sig0_%d" % h) for h in range(2)]
         for h in range(2):
-            if h == 1:
-                fetch(1)
-            c = slice(256 * h, 256 * (h + 1))
-            nc.tensor.matmul_mx(out=bank[h][:, 0:256], lhsT=wac[0][:, 0:P].bitcast(FP8X4), lhsT_scale=was[0][:, 0:P],
-                                rhs=vw[:, c].bitcast(FP8X4), rhs_scale=vs[:, c], start=True, stop=True)
-            nc.scalar.activation(h0[h][:], bank[h][:, 0:256], SIGMOID, scale=cols[:, 0:1])
+            c = slice(HALF_LIST * h, HALF_LIST * (h + 1))
+            nc.vector.tensor_copy(v_w[:, c], tab_w[:].indirect(lists[0][:, 16 * h:16 * (h + 1)]))
+            nc.tensor.matmul_mx(out=bank[h][:, 0:HALF_LIST], lhsT=wa_w[0][:, 0:P].bitcast(FP8X4), lhsT_scale=wa_s[0][:, 0:P],
+                                rhs=v_w[:, c].bitcast(FP8X4), rhs_scale=v_s[:, c], start=True, stop=True)
+            nc.scalar.activation(sig0[h][:], bank[h][:, 0:HALF_LIST], SIGMOID, scale=gin_first[:, 0:1])
         encode(0)
 
-        zt = [[sb([P, 2048], BF16, "zt%d%d" % (b, h)) for h in range(2)] for b in range(2)]
-        zc = [[sb([P, 512], U32, "zc%d%d" % (b, h)) for h in range(2)] for b in range(2)]
-        zs = [[sb([P, 512], U8, "zs%d%d" % (b, h)) for h in range(2)] for b in range(2)]
-        wtc = [sb([P, 256], U32, "wtc%d" % s) for s in range(4)]
-        wts = [sb([P, 256], U8, "wts%d" % s) for s in range(4)]
-        pre_tag = {1: "h00", 2: "h01", 5: "wtin0", 6: "wtin1", 7: "zin0"}
+        z_t = [[sb([P, 4 * QUARTER], BF16, "z_t%d%d" % (b, q)) for q in range(4)] for b in range(2)]
+        z_w = [[sb([P, BANK], U32, "z_w%d%d" % (b, h)) for h in range(2)] for b in range(2)]
+        z_s = [[sb([P, BANK], U8, "z_s%d%d" % (b, h)) for h in range(2)] for b in range(2)]
+        back_w = [sb([P, 2 * P], U32, "back_w%d" % s) for s in range(NTILES)]
+        back_s = [sb([P, 2 * P], U8, "back_s%d" % s) for s in range(NTILES)]
 
-        early = sb([P, 3, S], F32, "early", "tabw")
+        weight_tag = {1: "gin_first", 2: "sig0_0", 5: "sig3", 6: "sig4", LAST: "z_in00"}
+        weight0 = sb([P, S], F32, "weight0", "tab_w")
+        weight34 = sb([P, 2, S], F32, "weight34", "wa_by_k1")
 
         def place(s):
-            pre = early[:, (0, 3, 4).index(s), :] if s in (0, 3, 4) else sb([P, S], F32, "pre%d" % s, pre_tag[s])
-            nc.vector.tensor_scalar(pre[:], wgs_t[:], cols[:, 8 + s:9 + s], -1.0, MULT, MULT)
-            pg = pages[s % NPAGE]
+            page = pages[s % PAGES]
+            gain = gain_cols[:, 8 + s:9 + s]
             if s == 0:
                 for h in range(2):
-                    nc.vector.tensor_tensor(pg[:].indirect(lists[1][:, 16 * h:16 * (h + 1)]), h0[h][:], pre[:, 256 * h:256 * (h + 1)], MULT)
+                    c = slice(HALF_LIST * h, HALF_LIST * (h + 1))
+                    nc.vector.tensor_scalar(weight0[:, c], wgs_t[:, c], gain, None, MULT)
+                    nc.vector.tensor_tensor(page[:].indirect(lists[1][:, 16 * h:16 * (h + 1)]), sig0[h][:], weight0[:, c], MULT)
+                return
+            weight = weight34[:, s - 3, :] if s in (3, 4) else sb([P, S], F32, "weight%d" % s, weight_tag[s])
+            if s in (3, 4, 5, 6):
+                nc.scalar.activation(weight[:], wgs_t[:], COPY, scale=gain)
             else:
-                nc.vector.tensor_tensor(pg[:].indirect(lists[1][:]), hs[s][:], pre[:], MULT)
+                nc.vector.tensor_scalar(weight[:], wgs_t[:], gain, None, MULT)
+            nc.vector.tensor_tensor(page[:].indirect(lists[1][:]), sig[s][:], weight[:], MULT)
 
-        def level1(s, last=False):
-            pg = pages[s % NPAGE]
-            b, sl = divmod(s, 4)
-            for h in range(2):
-                acc = bank[2 * (s % 2) + h]
-                for tb in range(4):
-                    c = slice(512 * h + P * tb, 512 * h + P * (tb + 1))
-                    nc.tensor.matmul(acc[:, P * tb:P * (tb + 1)], exp_t[s][:, c], ident[:], start=(tb == 0), stop=False, is_transpose=True)
-            for h in range(2):
-                acc = bank[2 * (s % 2) + h]
-                for tb in range(4):
-                    c = slice(512 * h + P * tb, 512 * h + P * (tb + 1))
-                    nc.tensor.matmul(acc[:, P * tb:P * (tb + 1)], pg[:, c], ident[:], start=False, stop=(tb == 3), is_transpose=True)
-                dst = zt[b][h][:].rearrange("c (u t q e) -> c u t q e", u=2, t=4, e=2)[:, :, :, 32 * sl:32 * sl + 32, :]
-                src = acc[:].rearrange("c (t q u e) -> c u t q e", t=4, u=2, e=2)
-                if last and h == 1:
-                    nc.vector.tensor_scalar(dst, src, -1.0, None, MULT)
-                else:
-                    nc.scalar.activation(dst, src, COPY, scale=-1.0)
+        def sum_slice(s):
+            page = pages[s % PAGES]
+            b, in_pass = divmod(s, 4)
+            blocks = 2 if s == LAST else 4
+            banks = [2, 3, 0, 1] if s == LAST else [2 * (s % 2), 2 * (s % 2) + 1]
+            for i, bk in enumerate(banks):
+                for tb in range(blocks):
+                    c = slice(P * (blocks * i + tb), P * (blocks * i + tb + 1))
+                    nc.tensor.matmul(bank[bk][:, P * tb:P * (tb + 1)], exp_t[s][:, c], ident[:],
+                                     start=(tb == 0), stop=False, is_transpose=True)
+            for i, bk in enumerate(banks):
+                for tb in range(blocks):
+                    c = slice(P * (blocks * i + tb), P * (blocks * i + tb + 1))
+                    nc.tensor.matmul(bank[bk][:, P * tb:P * (tb + 1)], page[:, c], ident[:],
+                                     start=False, stop=(tb == blocks - 1), is_transpose=True)
+                for g in range(blocks // 2):
+                    quarter = i if s == LAST else 2 * i + g
+                    dst = z_t[b][quarter][:].rearrange("c (u t q e) -> c u t q e", u=2, t=2, e=2)
+                    dst = dst[:, :, :, 32 * in_pass:32 * in_pass + 32, :]
+                    src = bank[bk][:, QUARTER * g:QUARTER * (g + 1)].rearrange("c (t q u e) -> c u t q e", t=2, u=2, e=2)
+                    if s == LAST and quarter % 2 == 1:
+                        nc.vector.tensor_scalar(dst, src, -1.0, None, MULT)
+                    else:
+                        nc.scalar.activation(dst, src, COPY, scale=-1.0)
 
-        def level2(b, banks, on_vector):
-            zin = sb([P, 4096], BF16, "zin%d" % b)
-            zw = zin[:].bitcast(F32)
+        def turn_back(b, banks):
             for h in range(2):
-                words = zt[b][h][:].bitcast(F32)
+                z_in = sb([P, 4 * BANK], BF16, "z_in%d%d" % (b, h))
                 for g in range(2):
-                    qd = 2 * h + g
-                    acc = bank[banks[qd]]
-                    for u in range(2):
-                        for t in range(2):
-                            o = 512 * u + P * (2 * g + t)
-                            nc.tensor.transpose(acc[:, 256 * u + P * t:256 * u + P * (t + 1)], words[:, o:o + P], ident[:])
-                    dst = zw[:, 512 * qd:512 * (qd + 1)].rearrange("p (c u) -> p c u", u=2)
+                    quarter = 2 * h + g
+                    words = z_t[b][quarter][:].bitcast(F32)
+                    acc = bank[banks[quarter]]
+                    for j in range(4):
+                        nc.tensor.transpose(acc[:, P * j:P * (j + 1)], words[:, P * j:P * (j + 1)], ident[:])
+                    dst = z_in[:].bitcast(F32)[:, BANK * g:BANK * (g + 1)].rearrange("p (c u) -> p c u", u=2)
                     src = acc[:].rearrange("p (u c) -> p c u", u=2)
-                    if qd in on_vector:
+                    if b == 1 and quarter == 1:
                         nc.vector.tensor_copy(dst, src)
                     else:
                         nc.scalar.copy(dst, src)
                     if b == 1:
-                        c = slice(256 * g, 256 * (g + 1))
-                        nc.vector.quantize_mx(out=zc[b][h][:, c].bitcast(FP8X4), scales=zs[b][h][:, c], in_=zin[:, 1024 * qd:1024 * (qd + 1)])
+                        c = slice(QUARTER * g, QUARTER * (g + 1))
+                        nc.vector.quantize_mx(out=z_w[b][h][:, c].bitcast(FP8X4), scales=z_s[b][h][:, c],
+                                              in_=z_in[:, 4 * QUARTER * g:4 * QUARTER * (g + 1)])
                 if b == 0:
-                    nc.vector.quantize_mx(out=zc[b][h][:].bitcast(FP8X4), scales=zs[b][h][:], in_=zin[:, 2048 * h:2048 * (h + 1)])
+                    nc.vector.quantize_mx(out=z_w[b][h][:].bitcast(FP8X4), scales=z_s[b][h][:], in_=z_in[:])
 
-        def back_weights(s):
-            wb = sb([P, H], BF16, "wb%d" % s, "h%d" % (1, 2, 5, 6)[s])
-            nc.scalar.copy(wb[:].rearrange("n (u q e) -> n u q e", u=2, e=2), wan[s][:].rearrange("n (q u e) -> n u q e", u=2, e=2))
-            words = wb[:].bitcast(F32)
+        def quantise_back(s, after_slice):
+            pairs = sb([P, H], BF16, "pairs%d" % s, "sig%d" % after_slice)
+            nc.scalar.copy(pairs[:].rearrange("n (u q e) -> n u q e", u=2, e=2),
+                           wa_by_n[s][:].rearrange("n (q u e) -> n u q e", u=2, e=2))
+            words = pairs[:].bitcast(F32)
             acc = bank[4 + s % 2]
             for b in range(2):
                 for u in range(2):
-                    o = 256 * u + P * b
-                    nc.tensor.transpose(acc[:, 256 * b + P * u:256 * b + P * (u + 1)], words[:, o:o + P], ident[:])
-            wtin = sb([P, H], BF16, "wtin%d" % s)
-            nc.scalar.copy(wtin[:].bitcast(F32).rearrange("p (b n u) -> p b n u", b=2, u=2),
+                    first = 2 * P * u + P * b
+                    nc.tensor.transpose(acc[:, P * (2 * b + u):P * (2 * b + u + 1)], words[:, first:first + P], ident[:])
+            back_in = sb([P, H], BF16, "back_in%d" % s)
+            nc.scalar.copy(back_in[:].bitcast(F32).rearrange("p (b n u) -> p b n u", b=2, u=2),
                            acc[:].rearrange("p (b u n) -> p b n u", b=2, u=2))
-            nc.vector.quantize_mx(out=wtc[s][:].bitcast(FP8X4), scales=wts[s][:], in_=wtin[:])
-
-        ybank = [(6, 7), (2, 3), (4, 5), (0, 1)]
+            nc.vector.quantize_mx(out=back_w[s][:].bitcast(FP8X4), scales=back_s[s][:], in_=back_in[:])
 
         def project(s, b, h):
-            acc = bank[ybank[s][h]]
+            acc = bank[Y_BANKS[s][h]]
             c = slice(P * b, P * (b + 1))
-            nc.tensor.matmul_mx(out=acc[:], lhsT=wtc[s][:, c].bitcast(FP8X4), lhsT_scale=wts[s][:, c],
-                                rhs=zc[b][h][:].bitcast(FP8X4), rhs_scale=zs[b][h][:], start=(b == 0), stop=False)
-            nc.tensor.matmul_mx(out=acc[:], lhsT=w4w[:, b, 256 * s:256 * (s + 1)].bitcast(FP4X4), lhsT_scale=w4s[:, b, P * s:P * (s + 1)],
-                                rhs=zc[b][h][:].bitcast(FP8X4), rhs_scale=zs[b][h][:], start=False, stop=(b == 1))
+            nc.tensor.matmul_mx(out=acc[:], lhsT=back_w[s][:, c].bitcast(FP8X4), lhsT_scale=back_s[s][:, c],
+                                rhs=z_w[b][h][:].bitcast(FP8X4), rhs_scale=z_s[b][h][:], start=(b == 0), stop=False)
+            nc.tensor.matmul_mx(out=acc[:], lhsT=w4_w[:, b, 2 * P * s:2 * P * (s + 1)].bitcast(FP4X4),
+                                lhsT_scale=w4_s[:, b, P * s:P * (s + 1)],
+                                rhs=z_w[b][h][:].bitcast(FP8X4), rhs_scale=z_s[b][h][:], start=False, stop=(b == 1))
 
         for s in range(4):
             place(s)
             if s == 0:
                 for i in (1, 2):
-                    quant_wak(i)
+                    quantise_wa(i)
                     encode(i)
-            level1(s)
+            sum_slice(s)
             if s >= 2:
-                back_weights(s - 2)
-        level2(0, [4, 5, 4, 5], [])
-        for s in range(4, 7):
+                quantise_back(s - 2, after_slice=s - 1)
+        turn_back(0, [4, 5, 4, 5])
+
+        for s in range(4, LAST):
             place(s)
-            level1(s)
+            sum_slice(s)
             if s >= 5:
-                back_weights(s - 3)
-        nc.tensor.transpose(bank[4][:, 0:P], rows2[:], ident[:])
-        nc.scalar.copy(cols2[:, 0:4], bank[4][:, 0:4])
-        place(7)
+                quantise_back(s - 3, after_slice=s)
+        nc.tensor.transpose(bank[4][:, 0:P], gout_rows[:], ident[:])
+        nc.scalar.copy(gout_cols[:, 0:NTILES], bank[4][:, 0:NTILES])
+        place(LAST)
         project(0, 0, 0)
         project(0, 0, 1)
-        level1(7, last=True)
-        level2(1, [4, 5, 0, 1], [1])
+        sum_slice(LAST)
+        turn_back(1, [4, 5, 2, 3])
 
-        for s in range(4):
+        for s in range(NTILES):
             y = sb([P, T2], F32, "y%d" % s, "exp%d" % s)
             for h in range(2):
                 if s > 0:
                     project(s, 0, h)
                 project(s, 1, h)
-                nc.scalar.activation(y[:, 512 * h:512 * (h + 1)], bank[ybank[s][h]][:], COPY, scale=cols2[:, s:s + 1])
-            x = sb([P, W], F32, "x%d" % s, "h%d" % (s + 1))
+                nc.scalar.activation(y[:, BANK * h:BANK * (h + 1)], bank[Y_BANKS[s][h]][:], COPY, scale=gout_cols[:, s:s + 1])
+            x = sb([P, WATCHED], F32, "x%d" % s, "sig%d" % (s + 1))
             nc.vector.tensor_tensor(x[:], y[:].indirect(lists[2][:]), jobs_t[:, s, :], ADD)
-            o = outs[s % 2]
-            nc.vector.tensor_tensor(o[:].indirect(lists[3][:]), x[:], wgo_t[:], MULT)
-            nc.sync.dma_start(out=out[P * s:P * (s + 1), :], in_=o[:])
+            handset = handsets[s % 2]
+            nc.vector.tensor_tensor(handset[:].indirect(lists[3][:]), x[:], wgo_t[:], MULT)
+            nc.sync.dma_start(out=out[P * s:P * (s + 1), :], in_=handset[:])

@@ -26,8 +26,10 @@ QUARTER = 256
 SLICES, NTILES = H // P, K // P
 LAST = SLICES - 1
 PAGES = 3
-WA_PIECES = [(0, 2), (2, 4), (4, 8)]
-Y_BANKS = [(6, 7), (0, 1), (4, 5), (2, 3)]
+WA_PIECES = [(0, 1), (1, 2), (2, 4), (4, 6), (6, 8)]
+Y_BANKS = [(6, 7), (4, 5), (2, 3), (0, 1)]
+ENCODE_BANKS = [0, 2, 3, 0, 1, 2, 3, 2]
+LAST_BANKS = [2, 3, 0, 1]
 
 
 def tile_list_porter_dispatch_memory_kernel(tc, tab_words, tab_scales, offs, offs2, offs3, offs4, wa, gin, gup,
@@ -46,32 +48,32 @@ def tile_list_porter_dispatch_memory_kernel(tc, tab_words, tab_scales, offs, off
         tab_s = sb([P, T], U8, "tab_s")
         w4_w = sb([P, 2, 2 * K], U8, "w4_w")
         w4_s = sb([P, 2, K], U8, "w4_s")
-        gain_rows = sb([P, P], F32, "gain_rows")
+        gin_rows = sb([P, P], F32, "gin_rows")
+        gup_rows = sb([P, P], F32, "gup_rows")
         gout_rows = sb([P, P], F32, "gout_rows")
         gout_cols = sb([P, 8], F32, "gout_cols")
-        gain_cols = sb([P, 32], F32, "gain_cols")
+        gin_cols = sb([P, 8], F32, "gin_cols")
+        gup_cols = sb([P, 8], F32, "gup_cols")
         ident = sb([P, P], F32, "ident")
         warm = sb([P, 8], F32, "warm")
         pages = [sb([P, T2], F32, "page%d" % i) for i in range(PAGES)]
-        handsets = [sb([P, T2], F32, "handset%d" % i) for i in range(2)]
         wa_by_k = [sb([P, 4, P * (b - a)], F32, "wa_by_k%d" % i) for i, (a, b) in enumerate(WA_PIECES)]
-        wa_by_n = [sb([P, H], F32, "wa_by_n%d" % s) for s in range(NTILES)]
         exp_t = [sb([P, T2], F32, "exp%d" % s) for s in range(SLICES)]
         wgs_t = sb([P, S], F32, "wgs_t")
         wgo_t = sb([P, WATCHED], F32, "wgo_t")
         jobs_t = sb([P, NTILES, WATCHED], F32, "jobs_t")
+        handsets = {}
 
+        nc.gpsimd.memset(gin_rows[:], 0.0)
+        nc.gpsimd.memset(tab_s[:].bitcast(U32), 0)
         nc.gpsimd.memset(ident[:], 0.0)
-        nc.gpsimd.memset(gain_rows[:], 0.0)
         make_identity(nc, ident[:], nomemset=True)
-        nc.vector.memset(tab_s[:].bitcast(I32), 0)
+        nc.vector.memset(gup_rows[:], 0.0)
         nc.vector.memset(pages[0][:], 0.0)
         nc.vector.memset(w4_s[:].rearrange("p a c -> p (a c)").bitcast(I32), 0)
         nc.vector.memset(gout_rows[:], 0.0)
         nc.vector.memset(pages[1][:], 0.0)
-        nc.vector.memset(handsets[0][:], 0.0)
         nc.gpsimd.memset(pages[2][:], 0.0)
-        nc.gpsimd.memset(handsets[1][:], 0.0)
 
         wa_k = wa.rearrange("(p j) r -> p j r", j=4)
 
@@ -82,36 +84,31 @@ def tile_list_porter_dispatch_memory_kernel(tc, tab_words, tab_scales, offs, off
         def load_expected(s):
             nc.sync.dma_start(out=exp_t[s][:], in_=expected[P * s:P * (s + 1), :])
 
-        def load_wa_by_n(s):
-            nc.sync.dma_start(out=wa_by_n[s][:], in_=wa[P * s:P * (s + 1), :])
-
         nc.sync.dma_start(lists[0][:], offs)
         load_wa_by_k(0)
-        nc.sync.dma_start(out=gain_rows[0:8, :], in_=gin.rearrange("(s p) -> s p", p=P))
-        nc.sync.dma_start(out=gain_rows[8:16, :], in_=gup.rearrange("(s p) -> s p", p=P))
+        nc.sync.dma_start(out=gin_rows[0:8, :], in_=gin.rearrange("(s p) -> s p", p=P))
         for q in range(4):
             nc.sync.dma_start(out=tab_s[32 * q:32 * q + 4, :].bitcast(I32), in_=tab_scales[0, 4 * q:4 * q + 4, :].bitcast(I32))
         nc.sync.dma_start(out=tab_w[:].bitcast(I32), in_=tab_words[0].rearrange("p t i -> p (t i)").bitcast(I32))
+        nc.sync.dma_start(out=gup_rows[0:8, :], in_=gup.rearrange("(s p) -> s p", p=P))
         nc.sync.dma_start(out=wgs_t[:], in_=wgs)
         nc.sync.dma_start(lists[1][:], offs2)
         load_wa_by_k(1)
         load_wa_by_k(2)
         load_expected(0)
+        load_wa_by_k(3)
         load_expected(1)
-        load_wa_by_n(0)
+        load_wa_by_k(4)
         load_expected(2)
-        load_wa_by_n(1)
         load_expected(3)
-        load_expected(4)
         nc.sync.dma_start(out=w4_w[:].bitcast(I32), in_=w4_words.rearrange("a p c -> p a c").bitcast(I32))
         for q in range(4):
             nc.sync.dma_start(out=w4_s[32 * q:32 * q + 4, :, :].bitcast(I32),
                               in_=w4_scales[:, 4 * q:4 * q + 4, :].rearrange("a r c -> r a c").bitcast(I32))
         nc.sync.dma_start(out=gout_rows[0:4, :], in_=gout.rearrange("(s p) -> s p", p=P))
+        load_expected(4)
         load_expected(5)
-        load_wa_by_n(2)
         load_expected(6)
-        load_wa_by_n(3)
         load_expected(7)
         nc.sync.dma_start(lists[2][:], offs3)
         nc.sync.dma_start(lists[3][:], offs4)
@@ -120,76 +117,56 @@ def tile_list_porter_dispatch_memory_kernel(tc, tab_words, tab_scales, offs, off
 
         nc.scalar.activation(warm[:, 0:1], ident[:, 0:1], SIGMOID)
 
-        nc.tensor.transpose(bank[0][:, 0:P], gain_rows[:], ident[:])
-        gin_first = sb([P, 2], F32, "gin_first")
-        nc.scalar.copy(gin_first[:], bank[0][:, 0:2])
-        nc.scalar.activation(gain_cols[:, 8:16], bank[0][:, 8:16], COPY, scale=-1.0)
-        nc.scalar.copy(gain_cols[:, 2:8], bank[0][:, 2:8])
+        nc.tensor.transpose(bank[0][:, 0:P], gin_rows[:], ident[:])
+        nc.scalar.copy(gin_cols[:], bank[0][:, 0:8])
+        nc.tensor.transpose(bank[1][:, 0:P], gup_rows[:], ident[:])
+        nc.scalar.activation(gup_cols[:], bank[1][:, 0:8], COPY, scale=-1.0)
 
         v_w = sb([P, S], U32, "v_w")
         v_s = sb([P, S], U8, "v_s")
         wa_w = [sb([P, P * (b - a)], U32, "wa_w%d" % i) for i, (a, b) in enumerate(WA_PIECES)]
         wa_s = [sb([P, P * (b - a)], U8, "wa_s%d" % i) for i, (a, b) in enumerate(WA_PIECES)]
-        sig = {s: sb([P, S], F32, "sig%d" % s) for s in range(1, SLICES)}
+        grouped = [sb([P, 4 * BANK], BF16, "wa_grouped%d" % b) for b in range(2)]
+        sig = {}
+        weight = {}
 
         def quantise_wa(i):
             a, b = WA_PIECES[i]
-            grouped = sb([P, 4 * P * (b - a)], BF16, "wa_grouped%d" % i, (None, "gin_first", "sig0_0")[i])
-            nc.scalar.copy(grouped[:].rearrange("p (c i j) -> p c j i", i=4, j=4),
+            piece = grouped[a // 4][:, 4 * P * (a % 4):4 * P * (a % 4 + b - a)]
+            nc.scalar.copy(piece.rearrange("p (c i j) -> p c j i", i=4, j=4),
                            wa_by_k[i][:].rearrange("p j (c i) -> p c j i", i=4))
-            nc.vector.quantize_mx(out=wa_w[i][:].bitcast(FP8X4), scales=wa_s[i][:], in_=grouped[:])
+            nc.vector.quantize_mx(out=wa_w[i][:].bitcast(FP8X4), scales=wa_s[i][:], in_=piece)
 
-        def encode(i):
-            a, b = WA_PIECES[i]
-            for s in range(max(a, 1), b):
-                c = slice(P * (s - a), P * (s - a + 1))
-                acc = bank[2 if s == 1 else 6 + s % 2]
-                nc.tensor.matmul_mx(out=acc[:], lhsT=wa_w[i][:, c].bitcast(FP8X4), lhsT_scale=wa_s[i][:, c],
-                                    rhs=v_w[:].bitcast(FP8X4), rhs_scale=v_s[:], start=True, stop=True)
-                nc.scalar.activation(sig[s][:], acc[:], SIGMOID, scale=(gin_first if s == 1 else gain_cols)[:, s:s + 1])
+        def encode(s, tag=None):
+            i = [n for n, (a, b) in enumerate(WA_PIECES) if a <= s < b][0]
+            c = slice(P * (s - WA_PIECES[i][0]), P * (s - WA_PIECES[i][0] + 1))
+            acc = bank[ENCODE_BANKS[s]]
+            sig[s] = sb([P, S], F32, "sig%d" % s, tag)
+            nc.tensor.matmul_mx(out=acc[:], lhsT=wa_w[i][:, c].bitcast(FP8X4), lhsT_scale=wa_s[i][:, c],
+                                rhs=v_w[:].bitcast(FP8X4), rhs_scale=v_s[:], start=True, stop=True)
+            nc.scalar.activation(sig[s][:], acc[:], SIGMOID, scale=gin_cols[:, s:s + 1])
 
-        nc.vector.tensor_copy(v_s[:], tab_s[:].indirect(lists[0][:]))
-        quantise_wa(0)
-        sig0 = [sb([P, HALF_LIST], F32, "sig0_%d" % h) for h in range(2)]
-        for h in range(2):
-            c = slice(HALF_LIST * h, HALF_LIST * (h + 1))
-            nc.vector.tensor_copy(v_w[:, c], tab_w[:].indirect(lists[0][:, 16 * h:16 * (h + 1)]))
-            nc.tensor.matmul_mx(out=bank[h][:, 0:HALF_LIST], lhsT=wa_w[0][:, 0:P].bitcast(FP8X4), lhsT_scale=wa_s[0][:, 0:P],
-                                rhs=v_w[:, c].bitcast(FP8X4), rhs_scale=v_s[:, c], start=True, stop=True)
-            nc.scalar.activation(sig0[h][:], bank[h][:, 0:HALF_LIST], SIGMOID, scale=gin_first[:, 0:1])
-        encode(0)
-
-        z_t = [[sb([P, 4 * QUARTER], BF16, "z_t%d%d" % (b, q)) for q in range(4)] for b in range(2)]
-        z_w = [[sb([P, BANK], U32, "z_w%d%d" % (b, h)) for h in range(2)] for b in range(2)]
-        z_s = [[sb([P, BANK], U8, "z_s%d%d" % (b, h)) for h in range(2)] for b in range(2)]
-        back_w = [sb([P, 2 * P], U32, "back_w%d" % s) for s in range(NTILES)]
-        back_s = [sb([P, 2 * P], U8, "back_s%d" % s) for s in range(NTILES)]
-
-        weight_tag = {1: "gin_first", 2: "sig0_0", 5: "sig3", 6: "sig4", LAST: "z_in00"}
-        weight0 = sb([P, S], F32, "weight0", "tab_w")
-        weight34 = sb([P, 2, S], F32, "weight34", "wa_by_k1")
+        def make_weight(s, tag=None):
+            weight[s] = sb([P, S], F32, "weight%d" % s, tag)
+            nc.scalar.activation(weight[s][:], wgs_t[:], COPY, scale=gup_cols[:, s:s + 1])
 
         def place(s):
-            page = pages[s % PAGES]
-            gain = gain_cols[:, 8 + s:9 + s]
-            if s == 0:
-                for h in range(2):
-                    c = slice(HALF_LIST * h, HALF_LIST * (h + 1))
-                    nc.vector.tensor_scalar(weight0[:, c], wgs_t[:, c], gain, None, MULT)
-                    nc.vector.tensor_tensor(page[:].indirect(lists[1][:, 16 * h:16 * (h + 1)]), sig0[h][:], weight0[:, c], MULT)
-                return
-            weight = weight34[:, s - 3, :] if s in (3, 4) else sb([P, S], F32, "weight%d" % s, weight_tag[s])
-            if s in (3, 4, 5, 6):
-                nc.scalar.activation(weight[:], wgs_t[:], COPY, scale=gain)
-            else:
-                nc.vector.tensor_scalar(weight[:], wgs_t[:], gain, None, MULT)
-            nc.vector.tensor_tensor(page[:].indirect(lists[1][:]), sig[s][:], weight[:], MULT)
+            nc.vector.tensor_tensor(pages[s % PAGES][:].indirect(lists[1][:]), sig[s][:], weight[s][:], MULT)
+
+        halves0 = [sb([P, 8 * QUARTER], BF16, "z_t0%d" % h) for h in range(2)]
+        quarters1 = [sb([P, 4 * QUARTER], BF16, "z_t1%d" % q) for q in range(4)]
+        z_w = [[sb([P, BANK], U32, "z_w%d%d" % (b, h)) for h in range(2)] for b in range(2)]
+        z_s = [[sb([P, BANK], U8, "z_s%d%d" % (b, h)) for h in range(2)] for b in range(2)]
+        back_in = [sb([P, 4 * K], BF16, "back_in%d" % b) for b in range(2)]
+        back_s = [sb([P, K], U8, "back_s%d" % b) for b in range(2)]
+        back_w = {}
 
         def sum_slice(s):
             page = pages[s % PAGES]
             b, in_pass = divmod(s, 4)
+            rows = slice(32 * in_pass, 32 * in_pass + 32)
             blocks = 2 if s == LAST else 4
-            banks = [2, 3, 0, 1] if s == LAST else [2 * (s % 2), 2 * (s % 2) + 1]
+            banks = LAST_BANKS if s == LAST else [4 + 2 * (s % 2), 5 + 2 * (s % 2)]
             for i, bk in enumerate(banks):
                 for tb in range(blocks):
                     c = slice(P * (blocks * i + tb), P * (blocks * i + tb + 1))
@@ -200,26 +177,34 @@ def tile_list_porter_dispatch_memory_kernel(tc, tab_words, tab_scales, offs, off
                     c = slice(P * (blocks * i + tb), P * (blocks * i + tb + 1))
                     nc.tensor.matmul(bank[bk][:, P * tb:P * (tb + 1)], page[:, c], ident[:],
                                      start=False, stop=(tb == blocks - 1), is_transpose=True)
+                if b == 0:
+                    dst = halves0[i][:].rearrange("c (g u t q e) -> c g u t q e", g=2, u=2, t=2, e=2)[:, :, :, :, rows, :]
+                    nc.scalar.copy(dst, bank[bk][:].rearrange("c (g t q u e) -> c g u t q e", g=2, t=2, u=2, e=2))
+                    continue
                 for g in range(blocks // 2):
                     quarter = i if s == LAST else 2 * i + g
-                    dst = z_t[b][quarter][:].rearrange("c (u t q e) -> c u t q e", u=2, t=2, e=2)
-                    dst = dst[:, :, :, 32 * in_pass:32 * in_pass + 32, :]
+                    dst = quarters1[quarter][:].rearrange("c (u t q e) -> c u t q e", u=2, t=2, e=2)[:, :, :, rows, :]
                     src = bank[bk][:, QUARTER * g:QUARTER * (g + 1)].rearrange("c (t q u e) -> c u t q e", t=2, u=2, e=2)
                     if s == LAST and quarter % 2 == 1:
-                        nc.vector.tensor_scalar(dst, src, -1.0, None, MULT)
+                        nc.vector.tensor_copy(dst, src)
                     else:
-                        nc.scalar.activation(dst, src, COPY, scale=-1.0)
+                        nc.scalar.copy(dst, src)
 
-        def turn_back(b, banks):
+        z_in = {}
+
+        def turn_back(b):
             for h in range(2):
-                z_in = sb([P, 4 * BANK], BF16, "z_in%d%d" % (b, h))
+                z_in[b, h] = sb([P, 4 * BANK], BF16, "z_in%d%d" % (b, h))
                 for g in range(2):
                     quarter = 2 * h + g
-                    words = z_t[b][quarter][:].bitcast(F32)
-                    acc = bank[banks[quarter]]
+                    if b == 0:
+                        words = halves0[h][:].bitcast(F32)[:, BANK * g:BANK * (g + 1)]
+                    else:
+                        words = quarters1[quarter][:].bitcast(F32)
+                    acc = bank[LAST_BANKS[quarter] if b == 1 else g]
                     for j in range(4):
                         nc.tensor.transpose(acc[:, P * j:P * (j + 1)], words[:, P * j:P * (j + 1)], ident[:])
-                    dst = z_in[:].bitcast(F32)[:, BANK * g:BANK * (g + 1)].rearrange("p (c u) -> p c u", u=2)
+                    dst = z_in[b, h][:].bitcast(F32)[:, BANK * g:BANK * (g + 1)].rearrange("p (c u) -> p c u", u=2)
                     src = acc[:].rearrange("p (u c) -> p c u", u=2)
                     if b == 1 and quarter == 1:
                         nc.vector.tensor_copy(dst, src)
@@ -228,67 +213,119 @@ def tile_list_porter_dispatch_memory_kernel(tc, tab_words, tab_scales, offs, off
                     if b == 1:
                         c = slice(QUARTER * g, QUARTER * (g + 1))
                         nc.vector.quantize_mx(out=z_w[b][h][:, c].bitcast(FP8X4), scales=z_s[b][h][:, c],
-                                              in_=z_in[:, 4 * QUARTER * g:4 * QUARTER * (g + 1)])
+                                              in_=z_in[b, h][:, 4 * QUARTER * g:4 * QUARTER * (g + 1)])
                 if b == 0:
-                    nc.vector.quantize_mx(out=z_w[b][h][:].bitcast(FP8X4), scales=z_s[b][h][:], in_=z_in[:])
+                    nc.vector.quantize_mx(out=z_w[b][h][:].bitcast(FP8X4), scales=z_s[b][h][:], in_=z_in[b, h][:])
 
-        def quantise_back(s, after_slice):
-            pairs = sb([P, H], BF16, "pairs%d" % s, "sig%d" % after_slice)
-            nc.scalar.copy(pairs[:].rearrange("n (u q e) -> n u q e", u=2, e=2),
-                           wa_by_n[s][:].rearrange("n (q u e) -> n u q e", u=2, e=2))
-            words = pairs[:].bitcast(F32)
-            acc = bank[4 + s % 2]
-            for b in range(2):
-                for u in range(2):
-                    first = 2 * P * u + P * b
-                    nc.tensor.transpose(acc[:, P * (2 * b + u):P * (2 * b + u + 1)], words[:, first:first + P], ident[:])
-            back_in = sb([P, H], BF16, "back_in%d" % s)
-            nc.scalar.copy(back_in[:].bitcast(F32).rearrange("p (b n u) -> p b n u", b=2, u=2),
-                           acc[:].rearrange("p (b u n) -> p b n u", b=2, u=2))
-            nc.vector.quantize_mx(out=back_w[s][:].bitcast(FP8X4), scales=back_s[s][:], in_=back_in[:])
+        def turn_wa(b, jj):
+            words = grouped[b][:].bitcast(F32)
+            acc = bank[jj]
+            for i in range(4):
+                nc.tensor.transpose(acc[:, P * i:P * (i + 1)], words[:, 2 * i + jj:2 * BANK:8], ident[:])
+            dst = back_in[b][:].rearrange("q (p jj e i) -> q p jj e i", jj=2, e=2, i=4)[:, :, jj, :, :]
+            nc.scalar.copy(dst, acc[:].bitcast(BF16).rearrange("q (i p e) -> q p e i", i=4, e=2))
+
+        def quantise_back(b, tag=None):
+            back_w[b] = sb([P, K], U32, "back_w%d" % b, tag)
+            nc.vector.quantize_mx(out=back_w[b][:].bitcast(FP8X4), scales=back_s[b][:], in_=back_in[b][:])
 
         def project(s, b, h):
             acc = bank[Y_BANKS[s][h]]
-            c = slice(P * b, P * (b + 1))
-            nc.tensor.matmul_mx(out=acc[:], lhsT=back_w[s][:, c].bitcast(FP8X4), lhsT_scale=back_s[s][:, c],
+            c = slice(P * s, P * (s + 1))
+            nc.tensor.matmul_mx(out=acc[:], lhsT=back_w[b][:, c].bitcast(FP8X4), lhsT_scale=back_s[b][:, c],
                                 rhs=z_w[b][h][:].bitcast(FP8X4), rhs_scale=z_s[b][h][:], start=(b == 0), stop=False)
             nc.tensor.matmul_mx(out=acc[:], lhsT=w4_w[:, b, 2 * P * s:2 * P * (s + 1)].bitcast(FP4X4),
                                 lhsT_scale=w4_s[:, b, P * s:P * (s + 1)],
                                 rhs=z_w[b][h][:].bitcast(FP8X4), rhs_scale=z_s[b][h][:], start=False, stop=(b == 1))
 
-        for s in range(4):
-            place(s)
-            if s == 0:
-                for i in (1, 2):
-                    quantise_wa(i)
-                    encode(i)
-            sum_slice(s)
-            if s >= 2:
-                quantise_back(s - 2, after_slice=s - 1)
-        turn_back(0, [4, 5, 4, 5])
-
-        for s in range(4, LAST):
-            place(s)
-            sum_slice(s)
-            if s >= 5:
-                quantise_back(s - 3, after_slice=s)
-        nc.tensor.transpose(bank[4][:, 0:P], gout_rows[:], ident[:])
-        nc.scalar.copy(gout_cols[:, 0:NTILES], bank[4][:, 0:NTILES])
+        nc.vector.tensor_copy(v_s[:], tab_s[:].indirect(lists[0][:]))
+        quantise_wa(0)
+        for h in range(2):
+            c = slice(HALF_LIST * h, HALF_LIST * (h + 1))
+            nc.vector.tensor_copy(v_w[:, c], tab_w[:].indirect(lists[0][:, 16 * h:16 * (h + 1)]))
+            nc.tensor.matmul_mx(out=bank[h][:, 0:HALF_LIST], lhsT=wa_w[0][:].bitcast(FP8X4), lhsT_scale=wa_s[0][:],
+                                rhs=v_w[:, c].bitcast(FP8X4), rhs_scale=v_s[:, c], start=True, stop=True)
+        weight01 = sb([P, 2, S], F32, "weight01", "tab_w")
+        for s in range(2):
+            nc.vector.tensor_scalar(weight01[:, s, :], wgs_t[:], gup_cols[:, s:s + 1], None, MULT)
+        weight[1] = weight01[:, 1, :]
+        for h in range(2):
+            if h == 1:
+                quantise_wa(1)
+            sig0 = sb([P, HALF_LIST], F32, "sig0_%d" % h, (None, "wa_by_k1")[h])
+            nc.scalar.activation(sig0[:], bank[h][:, 0:HALF_LIST], SIGMOID, scale=gin_cols[:, 0:1])
+            nc.vector.tensor_tensor(pages[0][:].indirect(lists[1][:, 16 * h:16 * (h + 1)]), sig0[:],
+                                    weight01[:, 0, HALF_LIST * h:HALF_LIST * (h + 1)], MULT)
+        quantise_wa(2)
+        encode(1, "wa_by_k2")
+        place(1)
+        encode(2)
+        make_weight(2)
+        place(2)
+        quantise_wa(3)
+        sum_slice(0)
+        encode(3)
+        make_weight(3, "wa_by_k3")
+        place(3)
+        quantise_wa(4)
+        sum_slice(1)
+        encode(4)
+        make_weight(4, "wa_by_k4")
+        place(4)
+        turn_wa(0, 0)
+        sum_slice(2)
+        encode(5)
+        make_weight(5)
+        place(5)
+        turn_wa(0, 1)
+        quantise_back(0)
+        sum_slice(3)
+        turn_back(0)
+        encode(6)
+        make_weight(6, "z_t01")
+        place(6)
+        turn_wa(1, 0)
+        sum_slice(4)
+        encode(LAST)
+        make_weight(LAST)
         place(LAST)
-        project(0, 0, 0)
-        project(0, 0, 1)
+        nc.tensor.transpose(bank[3][:, 0:P], gout_rows[:], ident[:])
+        nc.scalar.activation(gout_cols[:, 0:NTILES], bank[3][:, 0:NTILES], COPY, scale=-1.0)
+        sum_slice(5)
+        for h in range(2):
+            project(0, 0, h)
+        sum_slice(6)
+        for h in range(2):
+            project(1, 0, h)
+        turn_wa(1, 1)
+        quantise_back(1, "sig7")
         sum_slice(LAST)
-        turn_back(1, [4, 5, 2, 3])
+        turn_back(1)
+        for i in range(2):
+            handsets[i] = sb([P, T2], F32, "handset%d" % i, "z_in1%d" % (1 - i))
+            nc.vector.memset(handsets[i][:], 0.0)
+        y = {}
 
-        for s in range(NTILES):
-            y = sb([P, T2], F32, "y%d" % s, "exp%d" % s)
+        def finish_y(s):
+            y[s] = sb([P, T2], F32, "y%d" % s, "exp%d" % s)
             for h in range(2):
-                if s > 0:
+                if s > 1:
                     project(s, 0, h)
                 project(s, 1, h)
-                nc.scalar.activation(y[:, BANK * h:BANK * (h + 1)], bank[Y_BANKS[s][h]][:], COPY, scale=gout_cols[:, s:s + 1])
-            x = sb([P, WATCHED], F32, "x%d" % s, "sig%d" % (s + 1))
-            nc.vector.tensor_tensor(x[:], y[:].indirect(lists[2][:]), jobs_t[:, s, :], ADD)
+                nc.scalar.activation(y[s][:, BANK * h:BANK * (h + 1)], bank[Y_BANKS[s][h]][:], COPY, scale=gout_cols[:, s:s + 1])
+
+        def hand_out(s):
+            x = sb([P, WATCHED], F32, "x%d" % s)
+            nc.vector.tensor_tensor(x[:], y[s][:].indirect(lists[2][:]), jobs_t[:, s, :], ADD)
             handset = handsets[s % 2]
             nc.vector.tensor_tensor(handset[:].indirect(lists[3][:]), x[:], wgo_t[:], MULT)
             nc.sync.dma_start(out=out[P * s:P * (s + 1), :], in_=handset[:])
+
+        finish_y(0)
+        finish_y(1)
+        hand_out(0)
+        finish_y(2)
+        hand_out(1)
+        finish_y(3)
+        hand_out(2)
+        hand_out(3)

@@ -27,9 +27,9 @@ SLICES, NTILES = H // P, K // P
 LAST = SLICES - 1
 PAGES = 3
 WA_PIECES = [(0, 1), (1, 2), (2, 4), (4, 6), (6, 8)]
-Y_BANKS = [(6, 7), (4, 5), (2, 3), (0, 1)]
+Y_BANKS = [(2, 4), (6, 7), (0, 1), (2, 4)]
 ENCODE_BANKS = [0, 2, 3, 0, 1, 2, 3, 2]
-LAST_BANKS = [2, 3, 0, 1]
+LAST_BANKS = [6, 7, 0, 1]
 
 
 def tile_list_porter_dispatch_memory_kernel(tc, tab_words, tab_scales, offs, offs2, offs3, offs4, wa, gin, gup,
@@ -52,6 +52,7 @@ def tile_list_porter_dispatch_memory_kernel(tc, tab_words, tab_scales, offs, off
         gup_rows = sb([P, P], F32, "gup_rows")
         gout_rows = sb([P, P], F32, "gout_rows")
         gout_cols = sb([P, 8], F32, "gout_cols")
+        gout_last = sb([P, 8], F32, "gout_last")
         gin_cols = sb([P, 8], F32, "gin_cols")
         gup_cols = sb([P, 8], F32, "gup_cols")
         ident = sb([P, P], F32, "ident")
@@ -62,7 +63,7 @@ def tile_list_porter_dispatch_memory_kernel(tc, tab_words, tab_scales, offs, off
         wgs_t = sb([P, S], F32, "wgs_t")
         wgo_t = sb([P, WATCHED], F32, "wgo_t")
         jobs_t = sb([P, NTILES, WATCHED], F32, "jobs_t")
-        handsets = {}
+        handsets = {1: sb([P, T2], F32, "handset1")}
 
         nc.gpsimd.memset(gin_rows[:], 0.0)
         nc.gpsimd.memset(tab_s[:].bitcast(U32), 0)
@@ -73,7 +74,8 @@ def tile_list_porter_dispatch_memory_kernel(tc, tab_words, tab_scales, offs, off
         nc.vector.memset(w4_s[:].rearrange("p a c -> p (a c)").bitcast(I32), 0)
         nc.vector.memset(gout_rows[:], 0.0)
         nc.vector.memset(pages[1][:], 0.0)
-        nc.gpsimd.memset(pages[2][:], 0.0)
+        nc.vector.memset(pages[2][:], 0.0)
+        nc.vector.memset(handsets[1][:], 0.0)
 
         wa_k = wa.rearrange("(p j) r -> p j r", j=4)
 
@@ -155,7 +157,7 @@ def tile_list_porter_dispatch_memory_kernel(tc, tab_words, tab_scales, offs, off
 
         halves0 = [sb([P, 8 * QUARTER], BF16, "z_t0%d" % h) for h in range(2)]
         quarters1 = [sb([P, 4 * QUARTER], BF16, "z_t1%d" % q) for q in range(4)]
-        z_w = [[sb([P, BANK], U32, "z_w%d%d" % (b, h)) for h in range(2)] for b in range(2)]
+        z_w = {}
         z_s = [[sb([P, BANK], U8, "z_s%d%d" % (b, h)) for h in range(2)] for b in range(2)]
         back_in = [sb([P, 4 * K], BF16, "back_in%d" % b) for b in range(2)]
         back_s = [sb([P, K], U8, "back_s%d" % b) for b in range(2)]
@@ -165,8 +167,8 @@ def tile_list_porter_dispatch_memory_kernel(tc, tab_words, tab_scales, offs, off
             page = pages[s % PAGES]
             b, in_pass = divmod(s, 4)
             rows = slice(32 * in_pass, 32 * in_pass + 32)
-            blocks = 2 if s == LAST else 4
-            banks = LAST_BANKS if s == LAST else [4 + 2 * (s % 2), 5 + 2 * (s % 2)]
+            blocks = 4
+            banks = [0, 1] if s == LAST else [4 + 2 * (s % 2), 5 + 2 * (s % 2)]
             for i, bk in enumerate(banks):
                 for tb in range(blocks):
                     c = slice(P * (blocks * i + tb), P * (blocks * i + tb + 1))
@@ -182,44 +184,47 @@ def tile_list_porter_dispatch_memory_kernel(tc, tab_words, tab_scales, offs, off
                     nc.scalar.copy(dst, bank[bk][:].rearrange("c (g t q u e) -> c g u t q e", g=2, t=2, u=2, e=2))
                     continue
                 for g in range(blocks // 2):
-                    quarter = i if s == LAST else 2 * i + g
+                    quarter = 2 * i + g
                     dst = quarters1[quarter][:].rearrange("c (u t q e) -> c u t q e", u=2, t=2, e=2)[:, :, :, rows, :]
                     src = bank[bk][:, QUARTER * g:QUARTER * (g + 1)].rearrange("c (t q u e) -> c u t q e", t=2, u=2, e=2)
-                    if s == LAST and quarter % 2 == 1:
+                    if s == LAST and i == 1:
                         nc.vector.tensor_copy(dst, src)
                     else:
                         nc.scalar.copy(dst, src)
 
         z_in = {}
 
-        def turn_back(b):
-            for h in range(2):
-                z_in[b, h] = sb([P, 4 * BANK], BF16, "z_in%d%d" % (b, h))
-                for g in range(2):
-                    quarter = 2 * h + g
-                    if b == 0:
-                        words = halves0[h][:].bitcast(F32)[:, BANK * g:BANK * (g + 1)]
-                    else:
-                        words = quarters1[quarter][:].bitcast(F32)
-                    acc = bank[LAST_BANKS[quarter] if b == 1 else g]
-                    for j in range(4):
-                        nc.tensor.transpose(acc[:, P * j:P * (j + 1)], words[:, P * j:P * (j + 1)], ident[:])
-                    dst = z_in[b, h][:].bitcast(F32)[:, BANK * g:BANK * (g + 1)].rearrange("p (c u) -> p c u", u=2)
-                    src = acc[:].rearrange("p (u c) -> p c u", u=2)
-                    if b == 1 and quarter == 1:
-                        nc.vector.tensor_copy(dst, src)
-                    else:
-                        nc.scalar.copy(dst, src)
-                    if b == 1:
-                        c = slice(QUARTER * g, QUARTER * (g + 1))
-                        nc.vector.quantize_mx(out=z_w[b][h][:, c].bitcast(FP8X4), scales=z_s[b][h][:, c],
-                                              in_=z_in[b, h][:, 4 * QUARTER * g:4 * QUARTER * (g + 1)])
+        def turn_back(b, h):
+            z_in[b, h] = sb([P, 4 * BANK], BF16, "z_in%d%d" % (b, h))
+            if b == 1:
+                z_w[b, h] = sb([P, BANK], U32, "z_w%d%d" % (b, h))
+            for g in range(2):
+                quarter = 2 * h + g
                 if b == 0:
-                    nc.vector.quantize_mx(out=z_w[b][h][:].bitcast(FP8X4), scales=z_s[b][h][:], in_=z_in[b, h][:])
+                    words = halves0[h][:].bitcast(F32)[:, BANK * g:BANK * (g + 1)]
+                else:
+                    words = quarters1[quarter][:].bitcast(F32)
+                acc = bank[LAST_BANKS[quarter] if b == 1 else g]
+                for j in range(4):
+                    nc.tensor.transpose(acc[:, P * j:P * (j + 1)], words[:, P * j:P * (j + 1)], ident[:])
+                dst = z_in[b, h][:].bitcast(F32)[:, BANK * g:BANK * (g + 1)].rearrange("p (c u) -> p c u", u=2)
+                src = acc[:].rearrange("p (u c) -> p c u", u=2)
+                if b == 1 and quarter == 1:
+                    nc.vector.tensor_copy(dst, src)
+                else:
+                    nc.scalar.copy(dst, src)
+                if b == 1:
+                    c = slice(QUARTER * g, QUARTER * (g + 1))
+                    nc.vector.quantize_mx(out=z_w[b, h][:, c].bitcast(FP8X4), scales=z_s[b][h][:, c],
+                                          in_=z_in[b, h][:, 4 * QUARTER * g:4 * QUARTER * (g + 1)])
 
-        def turn_wa(b, jj):
+        def quantise_z0(h, tag=None):
+            z_w[0, h] = sb([P, BANK], U32, "z_w0%d" % h, tag)
+            nc.vector.quantize_mx(out=z_w[0, h][:].bitcast(FP8X4), scales=z_s[0][h][:], in_=z_in[0, h][:])
+
+        def turn_wa(b, jj, bk):
             words = grouped[b][:].bitcast(F32)
-            acc = bank[jj]
+            acc = bank[bk]
             for i in range(4):
                 nc.tensor.transpose(acc[:, P * i:P * (i + 1)], words[:, 2 * i + jj:2 * BANK:8], ident[:])
             dst = back_in[b][:].rearrange("q (p jj e i) -> q p jj e i", jj=2, e=2, i=4)[:, :, jj, :, :]
@@ -229,14 +234,22 @@ def tile_list_porter_dispatch_memory_kernel(tc, tab_words, tab_scales, offs, off
             back_w[b] = sb([P, K], U32, "back_w%d" % b, tag)
             nc.vector.quantize_mx(out=back_w[b][:].bitcast(FP8X4), scales=back_s[b][:], in_=back_in[b][:])
 
-        def project(s, b, h):
-            acc = bank[Y_BANKS[s][h]]
+        def y_bank(s, h, g):
+            return bank[5] if (s, h, g) == (0, 1, 1) else bank[Y_BANKS[s][h]]
+
+        def project(s, b, h, g=None):
+            first, width = (0, BANK) if g is None else (QUARTER * g, QUARTER)
+            acc = y_bank(s, h, g)
             c = slice(P * s, P * (s + 1))
-            nc.tensor.matmul_mx(out=acc[:], lhsT=back_w[b][:, c].bitcast(FP8X4), lhsT_scale=back_s[b][:, c],
-                                rhs=z_w[b][h][:].bitcast(FP8X4), rhs_scale=z_s[b][h][:], start=(b == 0), stop=False)
-            nc.tensor.matmul_mx(out=acc[:], lhsT=w4_w[:, b, 2 * P * s:2 * P * (s + 1)].bitcast(FP4X4),
-                                lhsT_scale=w4_s[:, b, P * s:P * (s + 1)],
-                                rhs=z_w[b][h][:].bitcast(FP8X4), rhs_scale=z_s[b][h][:], start=False, stop=(b == 1))
+            t = slice(first, first + width)
+            nc.tensor.matmul_mx(out=acc[:, 0:width], lhsT=back_w[b][:, c].bitcast(FP8X4), lhsT_scale=back_s[b][:, c],
+                                rhs=z_w[b, h][:, t].bitcast(FP8X4), rhs_scale=z_s[b][h][:, t], start=(b == 0), stop=False)
+            step = BANK if g is None else P
+            for o in range(0, width, step):
+                t = slice(first + o, first + o + step)
+                nc.tensor.matmul_mx(out=acc[:, o:o + step], lhsT=w4_w[:, b, 2 * P * s:2 * P * (s + 1)].bitcast(FP4X4),
+                                    lhsT_scale=w4_s[:, b, c], rhs=z_w[b, h][:, t].bitcast(FP8X4), rhs_scale=z_s[b][h][:, t],
+                                    start=False, stop=(b == 1 and o + step == width))
 
         nc.vector.tensor_copy(v_s[:], tab_s[:].indirect(lists[0][:]))
         quantise_wa(0)
@@ -272,60 +285,77 @@ def tile_list_porter_dispatch_memory_kernel(tc, tab_words, tab_scales, offs, off
         encode(4)
         make_weight(4, "wa_by_k4")
         place(4)
-        turn_wa(0, 0)
+        turn_wa(0, 0, 0)
         sum_slice(2)
         encode(5)
         make_weight(5)
         place(5)
-        turn_wa(0, 1)
+        nc.tensor.transpose(bank[3][:, 0:P], gout_rows[:], ident[:])
+        nc.scalar.activation(gout_cols[:, 0:NTILES - 1], bank[3][:, 0:NTILES - 1], COPY, scale=-1.0)
+        nc.scalar.activation(gout_last[:, 0:1], bank[3][:, NTILES - 1:NTILES], COPY, scale=-1.0)
+        turn_wa(0, 1, 1)
         quantise_back(0)
         sum_slice(3)
-        turn_back(0)
+        turn_back(0, 0)
+        quantise_z0(0)
         encode(6)
-        make_weight(6, "z_t01")
+        make_weight(6, "z_t00")
         place(6)
-        turn_wa(1, 0)
+        turn_back(0, 1)
+        turn_wa(1, 0, 0)
         sum_slice(4)
         encode(LAST)
         make_weight(LAST)
         place(LAST)
-        nc.tensor.transpose(bank[3][:, 0:P], gout_rows[:], ident[:])
-        nc.scalar.activation(gout_cols[:, 0:NTILES], bank[3][:, 0:NTILES], COPY, scale=-1.0)
         sum_slice(5)
-        for h in range(2):
-            project(0, 0, h)
+        turn_wa(1, 1, 3)
         sum_slice(6)
-        for h in range(2):
-            project(1, 0, h)
-        turn_wa(1, 1)
+        project(0, 0, 0)
+        quantise_z0(1, "weight7")
         quantise_back(1, "sig7")
         sum_slice(LAST)
-        turn_back(1)
-        for i in range(2):
-            handsets[i] = sb([P, T2], F32, "handset%d" % i, "z_in1%d" % (1 - i))
-            nc.vector.memset(handsets[i][:], 0.0)
-        y = {}
+        turn_back(1, 0)
+        turn_back(1, 1)
+        handsets[0] = sb([P, T2], F32, "handset0", "z_in11")
+        nc.vector.memset(handsets[0][:], 0.0)
+        y = [sb([P, T2], F32, "y%d" % s, "exp%d" % s) for s in range(NTILES)]
+        x = {}
 
-        def finish_y(s):
-            y[s] = sb([P, T2], F32, "y%d" % s, "exp%d" % s)
-            for h in range(2):
-                if s > 1:
-                    project(s, 0, h)
-                project(s, 1, h)
-                nc.scalar.activation(y[s][:, BANK * h:BANK * (h + 1)], bank[Y_BANKS[s][h]][:], COPY, scale=gout_cols[:, s:s + 1])
+        def bring_y(s, h, g=None):
+            first, width = (0, BANK) if g is None else (QUARTER * g, QUARTER)
+            gain = gout_last[:, 0:1] if s == NTILES - 1 else gout_cols[:, s:s + 1]
+            dst, src = y[s][:, BANK * h + first:BANK * h + first + width], y_bank(s, h, g)[:, 0:width]
+            if (s, h, g) == (0, 1, 1):
+                nc.vector.tensor_scalar(dst, src, gain, None, MULT)
+            else:
+                nc.scalar.activation(dst, src, COPY, scale=gain)
+
+        def pick(s, tag=None):
+            x[s] = sb([P, WATCHED], F32, "x%d" % s, tag)
+            nc.vector.tensor_tensor(x[s][:], y[s][:].indirect(lists[2][:]), jobs_t[:, s, :], ADD)
 
         def hand_out(s):
-            x = sb([P, WATCHED], F32, "x%d" % s)
-            nc.vector.tensor_tensor(x[:], y[s][:].indirect(lists[2][:]), jobs_t[:, s, :], ADD)
             handset = handsets[s % 2]
-            nc.vector.tensor_tensor(handset[:].indirect(lists[3][:]), x[:], wgo_t[:], MULT)
+            nc.vector.tensor_tensor(handset[:].indirect(lists[3][:]), x[s][:], wgo_t[:], MULT)
             nc.sync.dma_start(out=out[P * s:P * (s + 1), :], in_=handset[:])
 
-        finish_y(0)
-        finish_y(1)
+        for g in range(2):
+            project(0, 0, 1, g)
+        project(0, 1, 0)
+        bring_y(0, 0)
+        for g in range(2):
+            project(0, 1, 1, g)
+            bring_y(0, 1, g)
+        for s in range(1, NTILES):
+            for h in range(2):
+                project(s, 0, h)
+                project(s, 1, h)
+                bring_y(s, h)
+        pick(0)
+        pick(1)
         hand_out(0)
-        finish_y(2)
         hand_out(1)
-        finish_y(3)
+        pick(2, "gout_last")
+        pick(3)
         hand_out(2)
         hand_out(3)

@@ -27,7 +27,7 @@ SLICES, NTILES = H // P, K // P
 LAST = SLICES - 1
 PAGES = 3
 WA_PIECES = [(0, 1), (1, 2), (2, 4), (4, 6), (6, 8)]
-Y_BANKS = [(2, 4), (6, 7), (0, 1), (2, 4)]
+Y_BANKS = [(2, 6), (4, 5), (0, 1), (2, 6)]
 ENCODE_BANKS = [0, 2, 3, 0, 1, 2, 3, 2]
 LAST_BANKS = [6, 7, 0, 1]
 
@@ -63,7 +63,7 @@ def tile_list_porter_dispatch_memory_kernel(tc, tab_words, tab_scales, offs, off
         wgs_t = sb([P, S], F32, "wgs_t")
         wgo_t = sb([P, WATCHED], F32, "wgo_t")
         jobs_t = sb([P, NTILES, WATCHED], F32, "jobs_t")
-        handsets = {1: sb([P, T2], F32, "handset1")}
+        handsets = [sb([P, T2], F32, "handset%d" % i) for i in range(2)]
 
         nc.gpsimd.memset(gin_rows[:], 0.0)
         nc.gpsimd.memset(tab_s[:].bitcast(U32), 0)
@@ -75,6 +75,7 @@ def tile_list_porter_dispatch_memory_kernel(tc, tab_words, tab_scales, offs, off
         nc.vector.memset(gout_rows[:], 0.0)
         nc.vector.memset(pages[1][:], 0.0)
         nc.vector.memset(pages[2][:], 0.0)
+        nc.vector.memset(handsets[0][:], 0.0)
         nc.vector.memset(handsets[1][:], 0.0)
 
         wa_k = wa.rearrange("(p j) r -> p j r", j=4)
@@ -230,19 +231,21 @@ def tile_list_porter_dispatch_memory_kernel(tc, tab_words, tab_scales, offs, off
             dst = back_in[b][:].rearrange("q (p jj e i) -> q p jj e i", jj=2, e=2, i=4)[:, :, jj, :, :]
             nc.scalar.copy(dst, acc[:].bitcast(BF16).rearrange("q (i p e) -> q p e i", i=4, e=2))
 
-        def quantise_back(b, tag=None):
-            back_w[b] = sb([P, K], U32, "back_w%d" % b, tag)
-            nc.vector.quantize_mx(out=back_w[b][:].bitcast(FP8X4), scales=back_s[b][:], in_=back_in[b][:])
+        def quantise_back(b, first, last, codes):
+            nc.vector.quantize_mx(out=codes.bitcast(FP8X4), scales=back_s[b][:, P * first:P * last],
+                                  in_=back_in[b][:, 4 * P * first:4 * P * last])
+            for s in range(first, last):
+                back_w[b, s] = codes[:, P * (s - first):P * (s - first + 1)]
 
         def y_bank(s, h, g):
-            return bank[5] if (s, h, g) == (0, 1, 1) else bank[Y_BANKS[s][h]]
+            return bank[7] if (s, h, g) == (0, 1, 1) else bank[Y_BANKS[s][h]]
 
         def project(s, b, h, g=None):
             first, width = (0, BANK) if g is None else (QUARTER * g, QUARTER)
             acc = y_bank(s, h, g)
             c = slice(P * s, P * (s + 1))
             t = slice(first, first + width)
-            nc.tensor.matmul_mx(out=acc[:, 0:width], lhsT=back_w[b][:, c].bitcast(FP8X4), lhsT_scale=back_s[b][:, c],
+            nc.tensor.matmul_mx(out=acc[:, 0:width], lhsT=back_w[b, s].bitcast(FP8X4), lhsT_scale=back_s[b][:, c],
                                 rhs=z_w[b, h][:, t].bitcast(FP8X4), rhs_scale=z_s[b][h][:, t], start=(b == 0), stop=False)
             step = BANK if g is None else P
             for o in range(0, width, step):
@@ -294,7 +297,8 @@ def tile_list_porter_dispatch_memory_kernel(tc, tab_words, tab_scales, offs, off
         nc.scalar.activation(gout_cols[:, 0:NTILES - 1], bank[3][:, 0:NTILES - 1], COPY, scale=-1.0)
         nc.scalar.activation(gout_last[:, 0:1], bank[3][:, NTILES - 1:NTILES], COPY, scale=-1.0)
         turn_wa(0, 1, 1)
-        quantise_back(0)
+        back_first = sb([P, P], U32, "back_first")
+        quantise_back(0, 0, 1, back_first[:])
         sum_slice(3)
         turn_back(0, 0)
         quantise_z0(0)
@@ -312,12 +316,14 @@ def tile_list_porter_dispatch_memory_kernel(tc, tab_words, tab_scales, offs, off
         sum_slice(6)
         project(0, 0, 0)
         quantise_z0(1, "weight7")
-        quantise_back(1, "sig7")
+        back_second = sb([P, K], U32, "back_second", "sig7")
+        quantise_back(1, 0, NTILES, back_second[:])
         sum_slice(LAST)
         turn_back(1, 0)
         turn_back(1, 1)
-        handsets[0] = sb([P, T2], F32, "handset0", "z_in11")
-        nc.vector.memset(handsets[0][:], 0.0)
+        back_rest = sb([P, K - P], U32, "back_rest", "z_in11")
+        quantise_back(0, 1, 2, back_rest[:, 0:P])
+        quantise_back(0, 2, NTILES, back_rest[:, P:])
         y = [sb([P, T2], F32, "y%d" % s, "exp%d" % s) for s in range(NTILES)]
         x = {}
 
@@ -325,10 +331,7 @@ def tile_list_porter_dispatch_memory_kernel(tc, tab_words, tab_scales, offs, off
             first, width = (0, BANK) if g is None else (QUARTER * g, QUARTER)
             gain = gout_last[:, 0:1] if s == NTILES - 1 else gout_cols[:, s:s + 1]
             dst, src = y[s][:, BANK * h + first:BANK * h + first + width], y_bank(s, h, g)[:, 0:width]
-            if (s, h, g) == (0, 1, 1):
-                nc.vector.tensor_scalar(dst, src, gain, None, MULT)
-            else:
-                nc.scalar.activation(dst, src, COPY, scale=gain)
+            nc.scalar.activation(dst, src, COPY, scale=gain)
 
         def pick(s, tag=None):
             x[s] = sb([P, WATCHED], F32, "x%d" % s, tag)

@@ -27,9 +27,10 @@ SLICES, NTILES = H // P, K // P
 LAST = SLICES - 1
 PAGES = 3
 WA_PIECES = [(0, 1), (1, 2), (2, 4), (4, 6), (6, 8)]
-Y_BANKS = [(2, 6), (4, 5), (0, 1), (2, 6)]
+WA_CODES = [(0, 1), (1, 2), (2, 4), (4, 5), (5, 6), (6, 8)]
+Y_BANKS = [(2, 6), (5, 0), (1, 3), (4, 2)]
 ENCODE_BANKS = [0, 2, 3, 0, 1, 2, 3, 2]
-LAST_BANKS = [6, 7, 0, 1]
+LAST_BANKS = [6, 7, 3, 4]
 
 
 def tile_list_porter_dispatch_memory_kernel(tc, tab_words, tab_scales, offs, offs2, offs3, offs4, wa, gin, gup,
@@ -50,17 +51,20 @@ def tile_list_porter_dispatch_memory_kernel(tc, tab_words, tab_scales, offs, off
         w4_s = sb([P, 2, K], U8, "w4_s")
         gin_rows = sb([P, P], F32, "gin_rows")
         gup_rows = sb([P, P], F32, "gup_rows")
+        gain_rows = sb([P, 2 * P], F32, "gain_rows")
+        gain_dealt = sb([P, 2 * P], F32, "gain_dealt")
         gout_rows = sb([P, P], F32, "gout_rows")
         gout_cols = sb([P, 8], F32, "gout_cols")
         gout_last = sb([P, 8], F32, "gout_last")
-        gin_cols = sb([P, 8], F32, "gin_cols")
-        gup_cols = sb([P, 8], F32, "gup_cols")
+        gin_cols = [sb([P, 8], F32, "gin_cols%d" % b) for b in range(2)]
+        gup_cols = [sb([P, 8], F32, "gup_cols%d" % b) for b in range(2)]
         ident = sb([P, P], F32, "ident")
         warm = sb([P, 8], F32, "warm")
         pages = [sb([P, T2], F32, "page%d" % i) for i in range(PAGES)]
         wa_by_k = [sb([P, 4, P * (b - a)], F32, "wa_by_k%d" % i) for i, (a, b) in enumerate(WA_PIECES)]
         exp_t = [sb([P, T2], F32, "exp%d" % s) for s in range(SLICES)]
         wgs_t = sb([P, S], F32, "wgs_t")
+        wgs_dealt = [sb([P, S], F32, "wgs_dealt%d" % u) for u in range(2)]
         wgo_t = sb([P, WATCHED], F32, "wgo_t")
         jobs_t = sb([P, NTILES, WATCHED], F32, "jobs_t")
         handsets = [sb([P, T2], F32, "handset%d" % i) for i in range(2)]
@@ -69,6 +73,7 @@ def tile_list_porter_dispatch_memory_kernel(tc, tab_words, tab_scales, offs, off
         nc.gpsimd.memset(tab_s[:].bitcast(U32), 0)
         nc.gpsimd.memset(ident[:], 0.0)
         make_identity(nc, ident[:], nomemset=True)
+        nc.gpsimd.memset(gain_rows[:], 0.0)
         nc.vector.memset(gup_rows[:], 0.0)
         nc.vector.memset(pages[0][:], 0.0)
         nc.vector.memset(w4_s[:].rearrange("p a c -> p (a c)").bitcast(I32), 0)
@@ -85,24 +90,37 @@ def tile_list_porter_dispatch_memory_kernel(tc, tab_words, tab_scales, offs, off
             nc.sync.dma_start(out=wa_by_k[i][:], in_=wa_k[:, :, P * a:P * b])
 
         def load_expected(s):
-            nc.sync.dma_start(out=exp_t[s][:], in_=expected[P * s:P * (s + 1), :])
+            if s < 4:
+                nc.sync.dma_start(out=exp_t[s][:], in_=expected[P * s:P * (s + 1), :])
+            else:
+                u, half = divmod(s - 4, 2)
+                rows = expected[BANK + 2 * P * half:BANK + 2 * P * (half + 1), :]
+                nc.sync.dma_start(out=exp_t[s][:], in_=rows.rearrange("(a u e) t -> u a e t", u=2, e=2)[u])
+
+        def load_wgs_dealt(u):
+            for half in range(2):
+                nc.sync.dma_start(out=wgs_dealt[u][64 * half:64 * (half + 1), :],
+                                  in_=wgs.rearrange("(a u e) j -> u a e j", u=2, e=2)[u])
 
         nc.sync.dma_start(lists[0][:], offs)
         load_wa_by_k(0)
-        nc.sync.dma_start(out=gin_rows[0:8, :], in_=gin.rearrange("(s p) -> s p", p=P))
+        nc.sync.dma_start(out=gin_rows[0:4, :], in_=gin[0:BANK].rearrange("(s p) -> s p", p=P))
         for q in range(4):
             nc.sync.dma_start(out=tab_s[32 * q:32 * q + 4, :].bitcast(I32), in_=tab_scales[0, 4 * q:4 * q + 4, :].bitcast(I32))
         nc.sync.dma_start(out=tab_w[:].bitcast(I32), in_=tab_words[0].rearrange("p t i -> p (t i)").bitcast(I32))
-        nc.sync.dma_start(out=gup_rows[0:8, :], in_=gup.rearrange("(s p) -> s p", p=P))
+        nc.sync.dma_start(out=gup_rows[0:4, :], in_=gup[0:BANK].rearrange("(s p) -> s p", p=P))
         nc.sync.dma_start(out=wgs_t[:], in_=wgs)
         nc.sync.dma_start(lists[1][:], offs2)
         load_wa_by_k(1)
         load_wa_by_k(2)
         load_expected(0)
+        nc.sync.dma_start(out=gain_rows[0:2, :], in_=gin[BANK:H].rearrange("(s p) -> s p", p=2 * P))
+        nc.sync.dma_start(out=gain_rows[2:4, :], in_=gup[BANK:H].rearrange("(s p) -> s p", p=2 * P))
         load_wa_by_k(3)
         load_expected(1)
         load_wa_by_k(4)
         load_expected(2)
+        load_wgs_dealt(0)
         load_expected(3)
         nc.sync.dma_start(out=w4_w[:].bitcast(I32), in_=w4_words.rearrange("a p c -> p a c").bitcast(I32))
         for q in range(4):
@@ -110,6 +128,7 @@ def tile_list_porter_dispatch_memory_kernel(tc, tab_words, tab_scales, offs, off
                               in_=w4_scales[:, 4 * q:4 * q + 4, :].rearrange("a r c -> r a c").bitcast(I32))
         nc.sync.dma_start(out=gout_rows[0:4, :], in_=gout.rearrange("(s p) -> s p", p=P))
         load_expected(4)
+        load_wgs_dealt(1)
         load_expected(5)
         load_expected(6)
         load_expected(7)
@@ -121,61 +140,84 @@ def tile_list_porter_dispatch_memory_kernel(tc, tab_words, tab_scales, offs, off
         nc.scalar.activation(warm[:, 0:1], ident[:, 0:1], SIGMOID)
 
         nc.tensor.transpose(bank[0][:, 0:P], gin_rows[:], ident[:])
-        nc.scalar.copy(gin_cols[:], bank[0][:, 0:8])
+        nc.scalar.copy(gin_cols[0][:, 0:4], bank[0][:, 0:4])
         nc.tensor.transpose(bank[1][:, 0:P], gup_rows[:], ident[:])
-        nc.scalar.activation(gup_cols[:], bank[1][:, 0:8], COPY, scale=-1.0)
+        nc.scalar.activation(gup_cols[0][:, 0:4], bank[1][:, 0:4], COPY, scale=-1.0)
+
+        def deal_gains(bk):
+            nc.scalar.copy(gain_dealt[:].rearrange("s (u a e) -> s u a e", u=2, e=2),
+                           gain_rows[:].rearrange("s (a u e) -> s u a e", u=2, e=2))
+            for u in range(2):
+                nc.tensor.transpose(bank[bk][:, P * u:P * (u + 1)], gain_dealt[:, P * u:P * (u + 1)], ident[:])
+            turned = bank[bk][:, 0:2 * P].rearrange("p (u s) -> p u s", u=2)
+            nc.scalar.copy(gin_cols[1][:, 0:4].rearrange("p (u h) -> p u h", u=2), turned[:, :, 0:2])
+            nc.scalar.activation(gup_cols[1][:, 0:4].rearrange("p (u h) -> p u h", u=2), turned[:, :, 2:4], COPY, scale=-1.0)
+
+        def gain(cols, s):
+            return cols[s // 4][:, s % 4:s % 4 + 1]
 
         v_w = sb([P, S], U32, "v_w")
         v_s = sb([P, S], U8, "v_s")
-        wa_w = [sb([P, P * (b - a)], U32, "wa_w%d" % i) for i, (a, b) in enumerate(WA_PIECES)]
-        wa_s = [sb([P, P * (b - a)], U8, "wa_s%d" % i) for i, (a, b) in enumerate(WA_PIECES)]
+        wa_w = [sb([P, P * (b - a)], U32, "wa_w%d" % i) for i, (a, b) in enumerate(WA_CODES)]
+        wa_s = [sb([P, P * (b - a)], U8, "wa_s%d" % i) for i, (a, b) in enumerate(WA_CODES)]
         grouped = [sb([P, 4 * BANK], BF16, "wa_grouped%d" % b) for b in range(2)]
         sig = {}
         weight = {}
 
-        def quantise_wa(i):
+        def group_wa(i):
             a, b = WA_PIECES[i]
-            piece = grouped[a // 4][:, 4 * P * (a % 4):4 * P * (a % 4 + b - a)]
-            nc.scalar.copy(piece.rearrange("p (c i j) -> p c j i", i=4, j=4),
-                           wa_by_k[i][:].rearrange("p j (c i) -> p c j i", i=4))
-            nc.vector.quantize_mx(out=wa_w[i][:].bitcast(FP8X4), scales=wa_s[i][:], in_=piece)
+            if a < 4:
+                piece = grouped[0][:, 4 * P * a:4 * P * b]
+                nc.scalar.copy(piece.rearrange("p (c i j) -> p c j i", i=4, j=4),
+                               wa_by_k[i][:].rearrange("p j (c i) -> p c j i", i=4))
+            else:
+                half = (a - 4) // 2
+                nc.scalar.copy(grouped[1][:].rearrange("p (u h a e j) -> p u h a j e", u=2, h=2, e=2, j=4)[:, :, half],
+                               wa_by_k[i][:].rearrange("p j (a u e) -> p u a j e", u=2, e=2))
+
+        def quantise_wa(i):
+            a, b = WA_CODES[i]
+            nc.vector.quantize_mx(out=wa_w[i][:].bitcast(FP8X4), scales=wa_s[i][:],
+                                  in_=grouped[a // 4][:, 4 * P * (a % 4):4 * P * (a % 4 + b - a)])
 
         def encode(s, tag=None):
-            i = [n for n, (a, b) in enumerate(WA_PIECES) if a <= s < b][0]
-            c = slice(P * (s - WA_PIECES[i][0]), P * (s - WA_PIECES[i][0] + 1))
+            i = [n for n, (a, b) in enumerate(WA_CODES) if a <= s < b][0]
+            c = slice(P * (s - WA_CODES[i][0]), P * (s - WA_CODES[i][0] + 1))
             acc = bank[ENCODE_BANKS[s]]
             sig[s] = sb([P, S], F32, "sig%d" % s, tag)
             nc.tensor.matmul_mx(out=acc[:], lhsT=wa_w[i][:, c].bitcast(FP8X4), lhsT_scale=wa_s[i][:, c],
                                 rhs=v_w[:].bitcast(FP8X4), rhs_scale=v_s[:], start=True, stop=True)
-            nc.scalar.activation(sig[s][:], acc[:], SIGMOID, scale=gin_cols[:, s:s + 1])
+            nc.scalar.activation(sig[s][:], acc[:], SIGMOID, scale=gain(gin_cols, s))
 
         def make_weight(s, tag=None):
             weight[s] = sb([P, S], F32, "weight%d" % s, tag)
-            nc.scalar.activation(weight[s][:], wgs_t[:], COPY, scale=gup_cols[:, s:s + 1])
+            rows = wgs_t if s < 4 else wgs_dealt[(s - 4) // 2]
+            nc.scalar.activation(weight[s][:], rows[:], COPY, scale=gain(gup_cols, s))
 
         def place(s):
             nc.vector.tensor_tensor(pages[s % PAGES][:].indirect(lists[1][:]), sig[s][:], weight[s][:], MULT)
 
         halves0 = [sb([P, 8 * QUARTER], BF16, "z_t0%d" % h) for h in range(2)]
-        quarters1 = [sb([P, 4 * QUARTER], BF16, "z_t1%d" % q) for q in range(4)]
+        early1 = [sb([P, 4 * QUARTER], BF16, "z_early%d" % h) for h in range(2)]
+        late1 = [sb([P, 2 * QUARTER], BF16, "z_late%d" % q) for q in range(4)]
         z_w = {}
         z_s = [[sb([P, BANK], U8, "z_s%d%d" % (b, h)) for h in range(2)] for b in range(2)]
         back_in = [sb([P, 4 * K], BF16, "back_in%d" % b) for b in range(2)]
         back_s = [sb([P, K], U8, "back_s%d" % b) for b in range(2)]
         back_w = {}
 
-        def sum_slice(s):
+        def sum_slice(s, expected_part=True, page_part=True):
             page = pages[s % PAGES]
             b, in_pass = divmod(s, 4)
             rows = slice(32 * in_pass, 32 * in_pass + 32)
             blocks = 4
             banks = [0, 1] if s == LAST else [4 + 2 * (s % 2), 5 + 2 * (s % 2)]
-            for i, bk in enumerate(banks):
+            for i, bk in enumerate(banks if expected_part else []):
                 for tb in range(blocks):
                     c = slice(P * (blocks * i + tb), P * (blocks * i + tb + 1))
                     nc.tensor.matmul(bank[bk][:, P * tb:P * (tb + 1)], exp_t[s][:, c], ident[:],
                                      start=(tb == 0), stop=False, is_transpose=True)
-            for i, bk in enumerate(banks):
+            for i, bk in enumerate(banks if page_part else []):
                 for tb in range(blocks):
                     c = slice(P * (blocks * i + tb), P * (blocks * i + tb + 1))
                     nc.tensor.matmul(bank[bk][:, P * tb:P * (tb + 1)], page[:, c], ident[:],
@@ -184,10 +226,14 @@ def tile_list_porter_dispatch_memory_kernel(tc, tab_words, tab_scales, offs, off
                     dst = halves0[i][:].rearrange("c (g u t q e) -> c g u t q e", g=2, u=2, t=2, e=2)[:, :, :, :, rows, :]
                     nc.scalar.copy(dst, bank[bk][:].rearrange("c (g t q u e) -> c g u t q e", g=2, t=2, u=2, e=2))
                     continue
+                u, half = divmod(in_pass, 2)
+                if u == 0:
+                    nc.scalar.copy(early1[i][:].rearrange("c (t h p) -> c t h p", t=4, h=2)[:, :, half, :],
+                                   bank[bk][:].rearrange("c (t p) -> c t p", t=4))
+                    continue
                 for g in range(blocks // 2):
-                    quarter = 2 * i + g
-                    dst = quarters1[quarter][:].rearrange("c (u t q e) -> c u t q e", u=2, t=2, e=2)[:, :, :, rows, :]
-                    src = bank[bk][:, QUARTER * g:QUARTER * (g + 1)].rearrange("c (t q u e) -> c u t q e", t=2, u=2, e=2)
+                    dst = late1[2 * i + g][:].rearrange("c (t h p) -> c t h p", t=2, h=2)[:, :, half, :]
+                    src = bank[bk][:, QUARTER * g:QUARTER * (g + 1)].rearrange("c (t p) -> c t p", t=2)
                     if s == LAST and i == 1:
                         nc.vector.tensor_copy(dst, src)
                     else:
@@ -195,19 +241,27 @@ def tile_list_porter_dispatch_memory_kernel(tc, tab_words, tab_scales, offs, off
 
         z_in = {}
 
+        def turn_early(quarter):
+            words = early1[quarter // 2][:].bitcast(F32)
+            for t in range(2):
+                block = 2 * (quarter % 2) + t
+                nc.tensor.transpose(bank[LAST_BANKS[quarter]][:, P * t:P * (t + 1)], words[:, P * block:P * (block + 1)], ident[:])
+
         def turn_back(b, h):
             z_in[b, h] = sb([P, 4 * BANK], BF16, "z_in%d%d" % (b, h))
             if b == 1:
                 z_w[b, h] = sb([P, BANK], U32, "z_w%d%d" % (b, h))
             for g in range(2):
                 quarter = 2 * h + g
+                acc = bank[LAST_BANKS[quarter] if b == 1 else g]
                 if b == 0:
                     words = halves0[h][:].bitcast(F32)[:, BANK * g:BANK * (g + 1)]
+                    for j in range(4):
+                        nc.tensor.transpose(acc[:, P * j:P * (j + 1)], words[:, P * j:P * (j + 1)], ident[:])
                 else:
-                    words = quarters1[quarter][:].bitcast(F32)
-                acc = bank[LAST_BANKS[quarter] if b == 1 else g]
-                for j in range(4):
-                    nc.tensor.transpose(acc[:, P * j:P * (j + 1)], words[:, P * j:P * (j + 1)], ident[:])
+                    words = late1[quarter][:].bitcast(F32)
+                    for t in range(2):
+                        nc.tensor.transpose(acc[:, P * (2 + t):P * (3 + t)], words[:, P * t:P * (t + 1)], ident[:])
                 dst = z_in[b, h][:].bitcast(F32)[:, BANK * g:BANK * (g + 1)].rearrange("p (c u) -> p c u", u=2)
                 src = acc[:].rearrange("p (u c) -> p c u", u=2)
                 if b == 1 and quarter == 1:
@@ -227,7 +281,11 @@ def tile_list_porter_dispatch_memory_kernel(tc, tab_words, tab_scales, offs, off
             words = grouped[b][:].bitcast(F32)
             acc = bank[bk]
             for i in range(4):
-                nc.tensor.transpose(acc[:, P * i:P * (i + 1)], words[:, 2 * i + jj:2 * BANK:8], ident[:])
+                if b == 0:
+                    rows = words[:, 2 * i + jj:2 * BANK:8]
+                else:
+                    rows = words[:, BANK * (i // 2) + 2 * (i % 2) + jj:BANK * (i // 2 + 1):4]
+                nc.tensor.transpose(acc[:, P * i:P * (i + 1)], rows, ident[:])
             dst = back_in[b][:].rearrange("q (p jj e i) -> q p jj e i", jj=2, e=2, i=4)[:, :, jj, :, :]
             nc.scalar.copy(dst, acc[:].bitcast(BF16).rearrange("q (i p e) -> q p e i", i=4, e=2))
 
@@ -255,6 +313,7 @@ def tile_list_porter_dispatch_memory_kernel(tc, tab_words, tab_scales, offs, off
                                     start=False, stop=(b == 1 and o + step == width))
 
         nc.vector.tensor_copy(v_s[:], tab_s[:].indirect(lists[0][:]))
+        group_wa(0)
         quantise_wa(0)
         for h in range(2):
             c = slice(HALF_LIST * h, HALF_LIST * (h + 1))
@@ -263,27 +322,33 @@ def tile_list_porter_dispatch_memory_kernel(tc, tab_words, tab_scales, offs, off
                                 rhs=v_w[:, c].bitcast(FP8X4), rhs_scale=v_s[:, c], start=True, stop=True)
         weight01 = sb([P, 2, S], F32, "weight01", "tab_w")
         for s in range(2):
-            nc.vector.tensor_scalar(weight01[:, s, :], wgs_t[:], gup_cols[:, s:s + 1], None, MULT)
+            nc.vector.tensor_scalar(weight01[:, s, :], wgs_t[:], gain(gup_cols, s), None, MULT)
         weight[1] = weight01[:, 1, :]
         for h in range(2):
             if h == 1:
+                group_wa(1)
                 quantise_wa(1)
             sig0 = sb([P, HALF_LIST], F32, "sig0_%d" % h, (None, "wa_by_k1")[h])
-            nc.scalar.activation(sig0[:], bank[h][:, 0:HALF_LIST], SIGMOID, scale=gin_cols[:, 0:1])
+            nc.scalar.activation(sig0[:], bank[h][:, 0:HALF_LIST], SIGMOID, scale=gain(gin_cols, 0))
             nc.vector.tensor_tensor(pages[0][:].indirect(lists[1][:, 16 * h:16 * (h + 1)]), sig0[:],
                                     weight01[:, 0, HALF_LIST * h:HALF_LIST * (h + 1)], MULT)
+        group_wa(2)
         quantise_wa(2)
         encode(1, "wa_by_k2")
         place(1)
         encode(2)
         make_weight(2)
         place(2)
+        deal_gains(1)
+        group_wa(3)
         quantise_wa(3)
         sum_slice(0)
         encode(3)
         make_weight(3, "wa_by_k3")
         place(3)
+        group_wa(4)
         quantise_wa(4)
+        quantise_wa(5)
         sum_slice(1)
         encode(4)
         make_weight(4, "wa_by_k4")
@@ -313,12 +378,16 @@ def tile_list_porter_dispatch_memory_kernel(tc, tab_words, tab_scales, offs, off
         place(LAST)
         sum_slice(5)
         turn_wa(1, 1, 3)
+        sum_slice(LAST, page_part=False)
         sum_slice(6)
         project(0, 0, 0)
+        for quarter in range(3):
+            turn_early(quarter)
         quantise_z0(1, "weight7")
         back_second = sb([P, K], U32, "back_second", "sig7")
         quantise_back(1, 0, NTILES, back_second[:])
-        sum_slice(LAST)
+        sum_slice(LAST, expected_part=False)
+        turn_early(3)
         turn_back(1, 0)
         turn_back(1, 1)
         back_rest = sb([P, K - P], U32, "back_rest", "z_in11")
@@ -329,9 +398,9 @@ def tile_list_porter_dispatch_memory_kernel(tc, tab_words, tab_scales, offs, off
 
         def bring_y(s, h, g=None):
             first, width = (0, BANK) if g is None else (QUARTER * g, QUARTER)
-            gain = gout_last[:, 0:1] if s == NTILES - 1 else gout_cols[:, s:s + 1]
+            column = gout_last[:, 0:1] if s == NTILES - 1 else gout_cols[:, s:s + 1]
             dst, src = y[s][:, BANK * h + first:BANK * h + first + width], y_bank(s, h, g)[:, 0:width]
-            nc.scalar.activation(dst, src, COPY, scale=gain)
+            nc.scalar.activation(dst, src, COPY, scale=column)
 
         def pick(s, tag=None):
             x[s] = sb([P, WATCHED], F32, "x%d" % s, tag)

@@ -28,7 +28,7 @@ LAST = SLICES - 1
 PAGES = 3
 WA_PIECES = [(0, 1), (1, 2), (2, 4), (4, 6), (6, 8)]
 WA_CODES = [(0, 1), (1, 2), (2, 4), (4, 5), (5, 6), (6, 8)]
-Y_BANKS = [(2, 6), (5, 0), (1, 3), (4, 2)]
+Y_BANKS = [(2, 5), (6, 7), (1, 3), (4, 2)]
 ENCODE_BANKS = [0, 2, 3, 0, 1, 2, 3, 2]
 LAST_BANKS = [6, 7, 3, 4]
 
@@ -49,15 +49,13 @@ def tile_list_porter_dispatch_memory_kernel(tc, tab_words, tab_scales, offs, off
         tab_s = sb([P, T], U8, "tab_s")
         w4_w = sb([P, 2, 2 * K], U8, "w4_w")
         w4_s = sb([P, 2, K], U8, "w4_s")
-        gin_rows = sb([P, P], F32, "gin_rows")
-        gup_rows = sb([P, P], F32, "gup_rows")
         gain_rows = sb([P, 2 * P], F32, "gain_rows")
         gain_dealt = sb([P, 2 * P], F32, "gain_dealt")
         gout_rows = sb([P, P], F32, "gout_rows")
         gout_cols = sb([P, 8], F32, "gout_cols")
         gout_last = sb([P, 8], F32, "gout_last")
-        gin_cols = [sb([P, 8], F32, "gin_cols%d" % b) for b in range(2)]
-        gup_cols = [sb([P, 8], F32, "gup_cols%d" % b) for b in range(2)]
+        gin_cols = sb([P, 4, 4], F32, "gin_cols")
+        gup_cols = sb([P, 4, 4], F32, "gup_cols")
         ident = sb([P, P], F32, "ident")
         warm = sb([P, 8], F32, "warm")
         pages = [sb([P, T2], F32, "page%d" % i) for i in range(PAGES)]
@@ -69,12 +67,10 @@ def tile_list_porter_dispatch_memory_kernel(tc, tab_words, tab_scales, offs, off
         jobs_t = sb([P, NTILES, WATCHED], F32, "jobs_t")
         handsets = [sb([P, T2], F32, "handset%d" % i) for i in range(2)]
 
-        nc.gpsimd.memset(gin_rows[:], 0.0)
+        nc.gpsimd.memset(gain_rows[:], 0.0)
         nc.gpsimd.memset(tab_s[:].bitcast(U32), 0)
         nc.gpsimd.memset(ident[:], 0.0)
         make_identity(nc, ident[:], nomemset=True)
-        nc.gpsimd.memset(gain_rows[:], 0.0)
-        nc.vector.memset(gup_rows[:], 0.0)
         nc.vector.memset(pages[0][:], 0.0)
         nc.vector.memset(w4_s[:].rearrange("p a c -> p (a c)").bitcast(I32), 0)
         nc.vector.memset(gout_rows[:], 0.0)
@@ -104,18 +100,16 @@ def tile_list_porter_dispatch_memory_kernel(tc, tab_words, tab_scales, offs, off
 
         nc.sync.dma_start(lists[0][:], offs)
         load_wa_by_k(0)
-        nc.sync.dma_start(out=gin_rows[0:4, :], in_=gin[0:BANK].rearrange("(s p) -> s p", p=P))
+        nc.sync.dma_start(out=gain_rows[0:4, :], in_=gin.rearrange("(s p) -> s p", p=2 * P))
+        nc.sync.dma_start(out=gain_rows[4:8, :], in_=gup.rearrange("(s p) -> s p", p=2 * P))
         for q in range(4):
             nc.sync.dma_start(out=tab_s[32 * q:32 * q + 4, :].bitcast(I32), in_=tab_scales[0, 4 * q:4 * q + 4, :].bitcast(I32))
         nc.sync.dma_start(out=tab_w[:].bitcast(I32), in_=tab_words[0].rearrange("p t i -> p (t i)").bitcast(I32))
-        nc.sync.dma_start(out=gup_rows[0:4, :], in_=gup[0:BANK].rearrange("(s p) -> s p", p=P))
         nc.sync.dma_start(out=wgs_t[:], in_=wgs)
         nc.sync.dma_start(lists[1][:], offs2)
         load_wa_by_k(1)
         load_wa_by_k(2)
         load_expected(0)
-        nc.sync.dma_start(out=gain_rows[0:2, :], in_=gin[BANK:H].rearrange("(s p) -> s p", p=2 * P))
-        nc.sync.dma_start(out=gain_rows[2:4, :], in_=gup[BANK:H].rearrange("(s p) -> s p", p=2 * P))
         load_wa_by_k(3)
         load_expected(1)
         load_wa_by_k(4)
@@ -139,22 +133,18 @@ def tile_list_porter_dispatch_memory_kernel(tc, tab_words, tab_scales, offs, off
 
         nc.scalar.activation(warm[:, 0:1], ident[:, 0:1], SIGMOID)
 
-        nc.tensor.transpose(bank[0][:, 0:P], gin_rows[:], ident[:])
-        nc.scalar.copy(gin_cols[0][:, 0:4], bank[0][:, 0:4])
-        nc.tensor.transpose(bank[1][:, 0:P], gup_rows[:], ident[:])
-        nc.scalar.activation(gup_cols[0][:, 0:4], bank[1][:, 0:4], COPY, scale=-1.0)
-
-        def deal_gains(bk):
-            nc.scalar.copy(gain_dealt[:].rearrange("s (u a e) -> s u a e", u=2, e=2),
-                           gain_rows[:].rearrange("s (a u e) -> s u a e", u=2, e=2))
-            for u in range(2):
-                nc.tensor.transpose(bank[bk][:, P * u:P * (u + 1)], gain_dealt[:, P * u:P * (u + 1)], ident[:])
-            turned = bank[bk][:, 0:2 * P].rearrange("p (u s) -> p u s", u=2)
-            nc.scalar.copy(gin_cols[1][:, 0:4].rearrange("p (u h) -> p u h", u=2), turned[:, :, 0:2])
-            nc.scalar.activation(gup_cols[1][:, 0:4].rearrange("p (u h) -> p u h", u=2), turned[:, :, 2:4], COPY, scale=-1.0)
+        nc.scalar.copy(gain_dealt[:].rearrange("s (u a e) -> s u a e", u=2, e=2),
+                       gain_rows[:].rearrange("s (a u e) -> s u a e", u=2, e=2))
+        for c in range(4):
+            source = (gain_rows, gain_dealt)[c // 2]
+            nc.tensor.transpose(bank[2][:, P * c:P * (c + 1)], source[:, P * (c % 2):P * (c % 2 + 1)], ident[:])
+        turned_gains = bank[2][:].rearrange("p (c s) -> p c s", c=4)
+        nc.scalar.copy(gin_cols[:], turned_gains[:, :, 0:4])
+        nc.scalar.activation(gup_cols[:], turned_gains[:, :, 4:8], COPY, scale=-1.0)
 
         def gain(cols, s):
-            return cols[s // 4][:, s % 4:s % 4 + 1]
+            c, row = (s % 2, s // 2) if s < 4 else (2 + (s - 4) // 2, 2 + s % 2)
+            return cols[:, c, row:row + 1]
 
         v_w = sb([P, S], U32, "v_w")
         v_s = sb([P, S], U8, "v_s")
@@ -296,7 +286,7 @@ def tile_list_porter_dispatch_memory_kernel(tc, tab_words, tab_scales, offs, off
                 back_w[b, s] = codes[:, P * (s - first):P * (s - first + 1)]
 
         def y_bank(s, h, g):
-            return bank[7] if (s, h, g) == (0, 1, 1) else bank[Y_BANKS[s][h]]
+            return bank[0] if (s, h, g) == (0, 1, 1) else bank[Y_BANKS[s][h]]
 
         def project(s, b, h, g=None):
             first, width = (0, BANK) if g is None else (QUARTER * g, QUARTER)
@@ -339,7 +329,6 @@ def tile_list_porter_dispatch_memory_kernel(tc, tab_words, tab_scales, offs, off
         encode(2)
         make_weight(2)
         place(2)
-        deal_gains(1)
         group_wa(3)
         quantise_wa(3)
         sum_slice(0)
@@ -400,7 +389,10 @@ def tile_list_porter_dispatch_memory_kernel(tc, tab_words, tab_scales, offs, off
             first, width = (0, BANK) if g is None else (QUARTER * g, QUARTER)
             column = gout_last[:, 0:1] if s == NTILES - 1 else gout_cols[:, s:s + 1]
             dst, src = y[s][:, BANK * h + first:BANK * h + first + width], y_bank(s, h, g)[:, 0:width]
-            nc.scalar.activation(dst, src, COPY, scale=column)
+            if (s, h, g) == (0, 1, 0):
+                nc.vector.tensor_scalar(dst, src, column, None, MULT)
+            else:
+                nc.scalar.activation(dst, src, COPY, scale=column)
 
         def pick(s, tag=None):
             x[s] = sb([P, WATCHED], F32, "x%d" % s, tag)

@@ -48,17 +48,16 @@ def tile_list_porter_dispatch_memory_kernel(tc, tab_words, tab_scales, offs, off
         tab_w = sb([P, T], U32, "tab_w")
         tab_s = sb([P, T], U8, "tab_s")
         w4_w = sb([P, 2, 2 * K], U8, "w4_w")
-        w4_s = sb([P, 2, K], U8, "w4_s")
         gain_rows = sb([P, 2 * P], F32, "gain_rows")
         gain_dealt = sb([P, 2 * P], F32, "gain_dealt")
-        gout_rows = sb([P, P], F32, "gout_rows")
+        gout_loaded = sb([P, NTILES], F32, "gout_loaded")
         gout_cols = sb([P, 8], F32, "gout_cols")
         gout_last = sb([P, 8], F32, "gout_last")
         gin_cols = sb([P, 4, 4], F32, "gin_cols")
         gup_cols = sb([P, 4, 4], F32, "gup_cols")
         ident = sb([P, P], F32, "ident")
         warm = sb([P, 8], F32, "warm")
-        pages = [sb([P, T2], F32, "page%d" % i) for i in range(PAGES)]
+        pages = [sb([P, T2 + (i == 0)], F32, "page%d" % i) for i in range(PAGES)]
         wa_by_k = [sb([P, 4, P * (b - a)], F32, "wa_by_k%d" % i) for i, (a, b) in enumerate(WA_PIECES)]
         exp_t = [sb([P, T2], F32, "exp%d" % s) for s in range(SLICES)]
         wgs_t = sb([P, S], F32, "wgs_t")
@@ -72,8 +71,6 @@ def tile_list_porter_dispatch_memory_kernel(tc, tab_words, tab_scales, offs, off
         nc.gpsimd.memset(ident[:], 0.0)
         make_identity(nc, ident[:], nomemset=True)
         nc.vector.memset(pages[0][:], 0.0)
-        nc.vector.memset(w4_s[:].rearrange("p a c -> p (a c)").bitcast(I32), 0)
-        nc.vector.memset(gout_rows[:], 0.0)
         nc.vector.memset(pages[1][:], 0.0)
         nc.vector.memset(pages[2][:], 0.0)
         nc.vector.memset(handsets[0][:], 0.0)
@@ -100,8 +97,8 @@ def tile_list_porter_dispatch_memory_kernel(tc, tab_words, tab_scales, offs, off
 
         nc.sync.dma_start(lists[0][:], offs)
         load_wa_by_k(0)
-        nc.sync.dma_start(out=gain_rows[0:4, :], in_=gin.rearrange("(s p) -> s p", p=2 * P))
-        nc.sync.dma_start(out=gain_rows[4:8, :], in_=gup.rearrange("(s p) -> s p", p=2 * P))
+        nc.sync.dma_start(out=gain_rows[8:12, :], in_=gin.rearrange("(s p) -> s p", p=2 * P))
+        nc.sync.dma_start(out=gain_rows[12:16, :], in_=gup.rearrange("(s p) -> s p", p=2 * P))
         for q in range(4):
             nc.sync.dma_start(out=tab_s[32 * q:32 * q + 4, :].bitcast(I32), in_=tab_scales[0, 4 * q:4 * q + 4, :].bitcast(I32))
         nc.sync.dma_start(out=tab_w[:].bitcast(I32), in_=tab_words[0].rearrange("p t i -> p (t i)").bitcast(I32))
@@ -116,11 +113,15 @@ def tile_list_porter_dispatch_memory_kernel(tc, tab_words, tab_scales, offs, off
         load_expected(2)
         load_wgs_dealt(0)
         load_expected(3)
+        v_s = sb([P, S], U8, "v_s")
+        nc.vector.tensor_copy(v_s[:], tab_s[:].indirect(lists[0][:]))
+        w4_s = sb([P, 2, K], U8, "w4_s", "tab_s")
         nc.sync.dma_start(out=w4_w[:].bitcast(I32), in_=w4_words.rearrange("a p c -> p a c").bitcast(I32))
         for q in range(4):
             nc.sync.dma_start(out=w4_s[32 * q:32 * q + 4, :, :].bitcast(I32),
                               in_=w4_scales[:, 4 * q:4 * q + 4, :].rearrange("a r c -> r a c").bitcast(I32))
-        nc.sync.dma_start(out=gout_rows[0:4, :], in_=gout.rearrange("(s p) -> s p", p=P))
+        with nc.allow_non_contiguous_dma(reason="gout, one value a partition"):
+            nc.sync.dma_start(out=gout_loaded[:], in_=gout.rearrange("(s p) -> p s", p=P))
         load_expected(4)
         load_wgs_dealt(1)
         load_expected(5)
@@ -139,15 +140,14 @@ def tile_list_porter_dispatch_memory_kernel(tc, tab_words, tab_scales, offs, off
             source = (gain_rows, gain_dealt)[c // 2]
             nc.tensor.transpose(bank[2][:, P * c:P * (c + 1)], source[:, P * (c % 2):P * (c % 2 + 1)], ident[:])
         turned_gains = bank[2][:].rearrange("p (c s) -> p c s", c=4)
-        nc.scalar.copy(gin_cols[:], turned_gains[:, :, 0:4])
-        nc.scalar.activation(gup_cols[:], turned_gains[:, :, 4:8], COPY, scale=-1.0)
+        nc.scalar.copy(gin_cols[:], turned_gains[:, :, 8:12])
+        nc.scalar.activation(gup_cols[:], turned_gains[:, :, 12:16], COPY, scale=-1.0)
 
         def gain(cols, s):
             c, row = (s % 2, s // 2) if s < 4 else (2 + (s - 4) // 2, 2 + s % 2)
             return cols[:, c, row:row + 1]
 
         v_w = sb([P, S], U32, "v_w")
-        v_s = sb([P, S], U8, "v_s")
         wa_w = [sb([P, P * (b - a)], U32, "wa_w%d" % i) for i, (a, b) in enumerate(WA_CODES)]
         wa_s = [sb([P, P * (b - a)], U8, "wa_s%d" % i) for i, (a, b) in enumerate(WA_CODES)]
         grouped = [sb([P, 4 * BANK], BF16, "wa_grouped%d" % b) for b in range(2)]
@@ -302,7 +302,6 @@ def tile_list_porter_dispatch_memory_kernel(tc, tab_words, tab_scales, offs, off
                                     lhsT_scale=w4_s[:, b, c], rhs=z_w[b, h][:, t].bitcast(FP8X4), rhs_scale=z_s[b][h][:, t],
                                     start=False, stop=(b == 1 and o + step == width))
 
-        nc.vector.tensor_copy(v_s[:], tab_s[:].indirect(lists[0][:]))
         group_wa(0)
         quantise_wa(0)
         for h in range(2):
@@ -310,7 +309,7 @@ def tile_list_porter_dispatch_memory_kernel(tc, tab_words, tab_scales, offs, off
             nc.vector.tensor_copy(v_w[:, c], tab_w[:].indirect(lists[0][:, 16 * h:16 * (h + 1)]))
             nc.tensor.matmul_mx(out=bank[h][:, 0:HALF_LIST], lhsT=wa_w[0][:].bitcast(FP8X4), lhsT_scale=wa_s[0][:],
                                 rhs=v_w[:, c].bitcast(FP8X4), rhs_scale=v_s[:, c], start=True, stop=True)
-        weight01 = sb([P, 2, S], F32, "weight01", "tab_w")
+        weight01 = sb([P, 2, S], F32, "weight01")
         for s in range(2):
             nc.vector.tensor_scalar(weight01[:, s, :], wgs_t[:], gain(gup_cols, s), None, MULT)
         weight[1] = weight01[:, 1, :]
@@ -347,9 +346,8 @@ def tile_list_porter_dispatch_memory_kernel(tc, tab_words, tab_scales, offs, off
         encode(5)
         make_weight(5)
         place(5)
-        nc.tensor.transpose(bank[3][:, 0:P], gout_rows[:], ident[:])
-        nc.scalar.activation(gout_cols[:, 0:NTILES - 1], bank[3][:, 0:NTILES - 1], COPY, scale=-1.0)
-        nc.scalar.activation(gout_last[:, 0:1], bank[3][:, NTILES - 1:NTILES], COPY, scale=-1.0)
+        nc.scalar.activation(gout_cols[:, 0:NTILES - 1], gout_loaded[:, 0:NTILES - 1], COPY, scale=-1.0)
+        nc.scalar.activation(gout_last[:, 0:1], gout_loaded[:, NTILES - 1:NTILES], COPY, scale=-1.0)
         turn_wa(0, 1, 1)
         back_first = sb([P, P], U32, "back_first")
         quantise_back(0, 0, 1, back_first[:])

@@ -100,7 +100,7 @@ def tile_list_porter_dispatch_memory_kernel(tc, tab_words, tab_scales, offs, off
         nc.sync.dma_start(out=gain_rows[8:12, :], in_=gin.rearrange("(s p) -> s p", p=2 * P))
         nc.sync.dma_start(out=gain_rows[12:16, :], in_=gup.rearrange("(s p) -> s p", p=2 * P))
         for q in range(4):
-            nc.sync.dma_start(out=tab_s[32 * q:32 * q + 4, :].bitcast(I32), in_=tab_scales[0, 4 * q:4 * q + 4, :].bitcast(I32))
+            nc.sync.dma_start(out=tab_s[q:P:32, :].bitcast(I32), in_=tab_scales[0, q:16:4, :].bitcast(I32))
         nc.sync.dma_start(out=tab_w[:].bitcast(I32), in_=tab_words[0].rearrange("p t i -> p (t i)").bitcast(I32))
         nc.sync.dma_start(out=wgs_t[:], in_=wgs)
         nc.sync.dma_start(lists[1][:], offs2)
@@ -288,19 +288,17 @@ def tile_list_porter_dispatch_memory_kernel(tc, tab_words, tab_scales, offs, off
         def y_bank(s, h, g):
             return bank[0] if (s, h, g) == (0, 1, 1) else bank[Y_BANKS[s][h]]
 
-        def project(s, b, h, g=None):
+        def project(s, b, h, g=None, alone=True):
             first, width = (0, BANK) if g is None else (QUARTER * g, QUARTER)
-            acc = y_bank(s, h, g)
+            at = 0 if alone else first
+            acc = y_bank(s, h, g)[:, at:at + width]
             c = slice(P * s, P * (s + 1))
             t = slice(first, first + width)
-            nc.tensor.matmul_mx(out=acc[:, 0:width], lhsT=back_w[b, s].bitcast(FP8X4), lhsT_scale=back_s[b][:, c],
+            nc.tensor.matmul_mx(out=acc, lhsT=back_w[b, s].bitcast(FP8X4), lhsT_scale=back_s[b][:, c],
                                 rhs=z_w[b, h][:, t].bitcast(FP8X4), rhs_scale=z_s[b][h][:, t], start=(b == 0), stop=False)
-            step = BANK if g is None else P
-            for o in range(0, width, step):
-                t = slice(first + o, first + o + step)
-                nc.tensor.matmul_mx(out=acc[:, o:o + step], lhsT=w4_w[:, b, 2 * P * s:2 * P * (s + 1)].bitcast(FP4X4),
-                                    lhsT_scale=w4_s[:, b, c], rhs=z_w[b, h][:, t].bitcast(FP8X4), rhs_scale=z_s[b][h][:, t],
-                                    start=False, stop=(b == 1 and o + step == width))
+            nc.tensor.matmul_mx(out=acc, lhsT=w4_w[:, b, 2 * P * s:2 * P * (s + 1)].bitcast(FP4X4),
+                                lhsT_scale=w4_s[:, b, c], rhs=z_w[b, h][:, t].bitcast(FP8X4), rhs_scale=z_s[b][h][:, t],
+                                start=False, stop=(b == 1 and (alone or g == 1)))
 
         group_wa(0)
         quantise_wa(0)
@@ -403,7 +401,8 @@ def tile_list_porter_dispatch_memory_kernel(tc, tab_words, tab_scales, offs, off
 
         for g in range(2):
             project(0, 0, 1, g)
-        project(0, 1, 0)
+        for g in range(2):
+            project(0, 1, 0, g, alone=False)
         bring_y(0, 0)
         for g in range(2):
             project(0, 1, 1, g)

@@ -57,7 +57,7 @@ def tile_list_porter_dispatch_memory_kernel(tc, tab_words, tab_scales, offs, off
         gup_cols = sb([P, 4, 4], F32, "gup_cols")
         ident = sb([P, P], F32, "ident")
         warm = sb([P, 8], F32, "warm")
-        pages = [sb([P, T2 + (i == 0)], F32, "page%d" % i) for i in range(PAGES)]
+        pages = [sb([P, T2], F32, "page%d" % i) for i in range(PAGES)]
         wa_by_k = [sb([P, 4, P * (b - a)], F32, "wa_by_k%d" % i) for i, (a, b) in enumerate(WA_PIECES)]
         exp_t = [sb([P, T2], F32, "exp%d" % s) for s in range(SLICES)]
         wgs_t = sb([P, S], F32, "wgs_t")

@@ -276,8 +276,8 @@ def tile_list_porter_dispatch_memory_kernel(tc, tab_words, tab_scales, offs, off
                 else:
                     rows = words[:, BANK * (i // 2) + 2 * (i % 2) + jj:BANK * (i // 2 + 1):4]
                 nc.tensor.transpose(acc[:, P * i:P * (i + 1)], rows, ident[:])
-            dst = back_in[b][:].rearrange("q (p jj e i) -> q p jj e i", jj=2, e=2, i=4)[:, :, jj, :, :]
-            nc.scalar.copy(dst, acc[:].bitcast(BF16).rearrange("q (i p e) -> q p e i", i=4, e=2))
+            dst = back_in[b][:].rearrange("q (p jj e i) -> q p jj i e", jj=2, e=2, i=4)[:, :, jj, :, :]
+            nc.scalar.copy(dst, acc[:].bitcast(BF16).rearrange("q (i p e) -> q p i e", i=4, e=2))
 
         def quantise_back(b, first, last, codes):
             nc.vector.quantize_mx(out=codes.bitcast(FP8X4), scales=back_s[b][:, P * first:P * last],

@@ -27,7 +27,7 @@ SLICES, NTILES = H // P, K // P
 LAST = SLICES - 1
 PAGES = 3
 WA_PIECES = [(0, 1), (1, 2), (2, 4), (4, 6), (6, 8)]
-WA_CODES = [(0, 1), (1, 2), (2, 4), (4, 5), (5, 6), (6, 8)]
+WA_CODES = [(0, 1), (1, 2), (2, 4), (4, 5), (5, 8)]
 Y_BANKS = [(2, 5), (6, 7), (1, 3), (4, 2)]
 ENCODE_BANKS = [0, 2, 3, 0, 1, 2, 3, 2]
 LAST_BANKS = [6, 7, 3, 4]
@@ -334,7 +334,6 @@ def tile_list_porter_dispatch_memory_kernel(tc, tab_words, tab_scales, offs, off
         place(3)
         group_wa(4)
         quantise_wa(4)
-        quantise_wa(5)
         sum_slice(1)
         encode(4)
         make_weight(4, "wa_by_k4")
@@ -369,15 +368,15 @@ def tile_list_porter_dispatch_memory_kernel(tc, tab_words, tab_scales, offs, off
         for quarter in range(3):
             turn_early(quarter)
         quantise_z0(1, "weight7")
-        back_second = sb([P, K], U32, "back_second", "sig7")
-        quantise_back(1, 0, NTILES, back_second[:])
+        back_second = sb([P, P], U32, "back_second", "sig7")
+        quantise_back(1, 0, 1, back_second[:])
         sum_slice(LAST, expected_part=False)
         turn_early(3)
         turn_back(1, 0)
         turn_back(1, 1)
-        back_rest = sb([P, K - P], U32, "back_rest", "z_in11")
-        quantise_back(0, 1, 2, back_rest[:, 0:P])
-        quantise_back(0, 2, NTILES, back_rest[:, P:])
+        back_rest = sb([P, 2, K - P], U32, "back_rest", "z_in11")
+        for b in range(2):
+            quantise_back(b, 1, NTILES, back_rest[:, b, :])
         y = [sb([P, T2], F32, "y%d" % s, "exp%d" % s) for s in range(NTILES)]
         x = {}
 
@@ -385,10 +384,7 @@ def tile_list_porter_dispatch_memory_kernel(tc, tab_words, tab_scales, offs, off
             first, width = (0, BANK) if g is None else (QUARTER * g, QUARTER)
             column = gout_last[:, 0:1] if s == NTILES - 1 else gout_cols[:, s:s + 1]
             dst, src = y[s][:, BANK * h + first:BANK * h + first + width], y_bank(s, h, g)[:, 0:width]
-            if (s, h, g) == (0, 1, 0):
-                nc.vector.tensor_scalar(dst, src, column, None, MULT)
-            else:
-                nc.scalar.activation(dst, src, COPY, scale=column)
+            nc.scalar.activation(dst, src, COPY, scale=column)
 
         def pick(s, tag=None):
             x[s] = sb([P, WATCHED], F32, "x%d" % s, tag)

@@ -66,6 +66,7 @@ def tile_list_porter_dispatch_memory_kernel(tc, tab_words, tab_scales, offs, off
         jobs_t = sb([P, NTILES, WATCHED], F32, "jobs_t")
         handsets = [sb([P, T2], F32, "handset%d" % i) for i in range(2)]
 
+        nc.gpsimd.memset(warm[:], 0.0)
         nc.gpsimd.memset(gain_rows[:], 0.0)
         nc.gpsimd.memset(tab_s[:].bitcast(U32), 0)
         nc.gpsimd.memset(ident[:], 0.0)
@@ -132,7 +133,7 @@ def tile_list_porter_dispatch_memory_kernel(tc, tab_words, tab_scales, offs, off
         nc.sync.dma_start(out=jobs_t[:], in_=jobs.rearrange("(s p) m -> p s m", p=P))
         nc.sync.dma_start(out=wgo_t[:], in_=wgo)
 
-        nc.scalar.activation(warm[:, 0:1], ident[:, 0:1], SIGMOID)
+        nc.scalar.activation(warm[:, 0:1], warm[:, 1:2], SIGMOID)
 
         nc.scalar.copy(gain_dealt[:].rearrange("s (u a e) -> s u a e", u=2, e=2),
                        gain_rows[:].rearrange("s (a u e) -> s u a e", u=2, e=2))

@@ -42,7 +42,7 @@ def tile_list_porter_dispatch_memory_kernel(tc, tab_words, tab_scales, offs, off
         bank = [psum.tile([P, BANK], F32, name="bank%d" % i) for i in range(8)]
 
         def sb(shape, dt, name, tag=None):
-            return keep.tile(shape, dt, name=name, tag=tag or name, align_bytes=64)
+            return keep.tile(shape, dt, name=name, tag=tag or name, align_bytes=256)
 
         lists = [keep.tile([P, S // 16], U16, name="list%d" % i) for i in range(4)]
         tab_w = sb([P, T], U32, "tab_w")

@@ -53,6 +53,7 @@ def tile_list_porter_dispatch_memory_kernel(tc, tab_words, tab_scales, offs, off
         gout_loaded = sb([P, NTILES], F32, "gout_loaded")
         gout_cols = sb([P, 8], F32, "gout_cols")
         gout_last = sb([P, 8], F32, "gout_last")
+        gout_first = sb([P, 8], F32, "gout_first")
         gin_cols = sb([P, 4, 4], F32, "gin_cols")
         gup_cols = sb([P, 4, 4], F32, "gup_cols")
         ident = sb([P, P], F32, "ident")
@@ -344,7 +345,8 @@ def tile_list_porter_dispatch_memory_kernel(tc, tab_words, tab_scales, offs, off
         encode(5)
         make_weight(5)
         place(5)
-        nc.scalar.activation(gout_cols[:, 0:NTILES - 1], gout_loaded[:, 0:NTILES - 1], COPY, scale=-1.0)
+        nc.scalar.activation(gout_cols[:, 1:NTILES - 1], gout_loaded[:, 1:NTILES - 1], COPY, scale=-1.0)
+        nc.scalar.activation(gout_first[:, 0:1], gout_loaded[:, 0:1], COPY, scale=-1.0)
         nc.scalar.activation(gout_last[:, 0:1], gout_loaded[:, NTILES - 1:NTILES], COPY, scale=-1.0)
         turn_wa(0, 1, 1)
         back_first = sb([P, P], U32, "back_first")
@@ -383,7 +385,7 @@ def tile_list_porter_dispatch_memory_kernel(tc, tab_words, tab_scales, offs, off
 
         def bring_y(s, h, g=None):
             first, width = (0, BANK) if g is None else (QUARTER * g, QUARTER)
-            column = gout_last[:, 0:1] if s == NTILES - 1 else gout_cols[:, s:s + 1]
+            column = {0: gout_first[:, 0:1], NTILES - 1: gout_last[:, 0:1]}.get(s, gout_cols[:, s:s + 1])
             dst, src = y[s][:, BANK * h + first:BANK * h + first + width], y_bank(s, h, g)[:, 0:width]
             nc.scalar.activation(dst, src, COPY, scale=column)
 
@@ -409,9 +411,16 @@ def tile_list_porter_dispatch_memory_kernel(tc, tab_words, tab_scales, offs, off
                 project(s, 0, h)
                 project(s, 1, h)
                 bring_y(s, h)
-        pick(0)
+        wgo_late = sb([P, HALF_LIST], F32, "wgo_late", "gout_first")
+        nc.sync.dma_start(out=wgo_late[:], in_=wgo[:, HALF_LIST:WATCHED])
+        x0 = [sb([P, HALF_LIST], F32, "x0_%d" % h) for h in range(2)]
+        for h in range(2):
+            nc.vector.tensor_tensor(x0[h][:], y[0][:].indirect(lists[2][:, 16 * h:16 * (h + 1)]),
+                                    jobs_t[:, 0, HALF_LIST * h:HALF_LIST * (h + 1)], ADD)
+        nc.vector.tensor_tensor(handsets[0][:].indirect(lists[3][:, 0:16]), x0[0][:], wgo_t[:, 0:HALF_LIST], MULT)
         pick(1)
-        hand_out(0)
+        nc.vector.tensor_tensor(handsets[0][:].indirect(lists[3][:, 16:32]), x0[1][:], wgo_late[:], MULT)
+        nc.sync.dma_start(out=out[0:P, :], in_=handsets[0][:])
         hand_out(1)
         pick(2, "gout_last")
         pick(3)

@@ -22,6 +22,7 @@ SIGMOID = mybir.ActivationFunctionType.Sigmoid
 P = 128
 BANK = 512
 HALF_LIST = 256
+FIRST = 128
 QUARTER = 256
 SLICES, NTILES = H // P, K // P
 LAST = SLICES - 1
@@ -54,6 +55,7 @@ def tile_list_porter_dispatch_memory_kernel(tc, tab_words, tab_scales, offs, off
         gout_cols = sb([P, 8], F32, "gout_cols")
         gout_last = sb([P, 8], F32, "gout_last")
         gout_first = sb([P, 8], F32, "gout_first")
+        gin_first = [sb([P, 8], F32, "gin_first%d" % h) for h in range(2)]
         gin_cols = sb([P, 4, 4], F32, "gin_cols")
         gup_cols = sb([P, 4, 4], F32, "gup_cols")
         ident = sb([P, P], F32, "ident")
@@ -142,6 +144,8 @@ def tile_list_porter_dispatch_memory_kernel(tc, tab_words, tab_scales, offs, off
             source = (gain_rows, gain_dealt)[c // 2]
             nc.tensor.transpose(bank[2][:, P * c:P * (c + 1)], source[:, P * (c % 2):P * (c % 2 + 1)], ident[:])
         turned_gains = bank[2][:].rearrange("p (c s) -> p c s", c=4)
+        for h in range(2):
+            nc.scalar.copy(gin_first[h][:, 0:1], turned_gains[:, 0, 8:9])
         nc.scalar.copy(gin_cols[:], turned_gains[:, :, 8:12])
         nc.scalar.activation(gup_cols[:], turned_gains[:, :, 12:16], COPY, scale=-1.0)
 
@@ -304,29 +308,29 @@ def tile_list_porter_dispatch_memory_kernel(tc, tab_words, tab_scales, offs, off
 
         group_wa(0)
         quantise_wa(0)
-        for h in range(2):
-            c = slice(HALF_LIST * h, HALF_LIST * (h + 1))
-            nc.vector.tensor_copy(v_w[:, c], tab_w[:].indirect(lists[0][:, 16 * h:16 * (h + 1)]))
-            nc.tensor.matmul_mx(out=bank[h][:, 0:HALF_LIST], lhsT=wa_w[0][:].bitcast(FP8X4), lhsT_scale=wa_s[0][:],
-                                rhs=v_w[:, c].bitcast(FP8X4), rhs_scale=v_s[:, c], start=True, stop=True)
-        weight01 = sb([P, 2, S], F32, "weight01")
-        for s in range(2):
-            nc.vector.tensor_scalar(weight01[:, s, :], wgs_t[:], gain(gup_cols, s), None, MULT)
-        weight[1] = weight01[:, 1, :]
-        for h in range(2):
+        pieces = [(0, FIRST), (FIRST, S)]
+        for h, (a, b) in enumerate(pieces):
+            nc.vector.tensor_copy(v_w[:, a:b], tab_w[:].indirect(lists[0][:, a // 16:b // 16]))
+            for c in ([slice(0, FIRST)], [slice(FIRST, 2 * FIRST), slice(2 * FIRST, S)])[h]:
+                nc.tensor.matmul_mx(out=bank[h][:, c], lhsT=wa_w[0][:].bitcast(FP8X4), lhsT_scale=wa_s[0][:],
+                                    rhs=v_w[:, c].bitcast(FP8X4), rhs_scale=v_s[:, c], start=True, stop=True)
+        weight[0] = sb([P, S], F32, "weight0")
+        nc.vector.tensor_scalar(weight[0][:], wgs_t[:], gain(gup_cols, 0), None, MULT)
+        for h, (a, b) in enumerate(pieces):
             if h == 1:
+                weight[1] = sb([P, S], F32, "weight1", "gin_first0")
+                nc.vector.tensor_scalar(weight[1][:], wgs_t[:], gain(gup_cols, 1), None, MULT)
                 group_wa(1)
                 quantise_wa(1)
-            sig0 = sb([P, HALF_LIST], F32, "sig0_%d" % h, (None, "wa_by_k1")[h])
-            nc.scalar.activation(sig0[:], bank[h][:, 0:HALF_LIST], SIGMOID, scale=gain(gin_cols, 0))
-            nc.vector.tensor_tensor(pages[0][:].indirect(lists[1][:, 16 * h:16 * (h + 1)]), sig0[:],
-                                    weight01[:, 0, HALF_LIST * h:HALF_LIST * (h + 1)], MULT)
+            sig0 = sb([P, b - a], F32, "sig0_%d" % h, (None, "wa_by_k1")[h])
+            nc.scalar.activation(sig0[:], bank[h][:, a:b], SIGMOID, scale=gin_first[h][:, 0:1])
+            nc.vector.tensor_tensor(pages[0][:].indirect(lists[1][:, a // 16:b // 16]), sig0[:], weight[0][:, a:b], MULT)
         group_wa(2)
         quantise_wa(2)
         encode(1, "wa_by_k2")
         place(1)
         encode(2)
-        make_weight(2)
+        make_weight(2, "gin_first1")
         place(2)
         group_wa(3)
         quantise_wa(3)
@@ -370,8 +374,8 @@ def tile_list_porter_dispatch_memory_kernel(tc, tab_words, tab_scales, offs, off
         project(0, 0, 0)
         for quarter in range(3):
             turn_early(quarter)
-        quantise_z0(1, "weight7")
-        back_second = sb([P, P], U32, "back_second", "sig7")
+        quantise_z0(1, "z_early0")
+        back_second = sb([P, P], U32, "back_second")
         quantise_back(1, 0, 1, back_second[:])
         sum_slice(LAST, expected_part=False)
         turn_early(3)

@@ -39,6 +39,7 @@ def tile_list_porter_dispatch_memory_kernel(tc, tab_words, tab_scales, offs, off
     nc = tc.nc
     with ExitStack() as ctx:
         keep = ctx.enter_context(tc.tile_pool(name="keep", bufs=1))
+        laid = ctx.enter_context(tc.tile_pool(name="laid", bufs=1))
         psum = ctx.enter_context(tc.psum_pool(name="psum", bufs=1))
         bank = [psum.tile([P, BANK], F32, name="bank%d" % i) for i in range(8)]
 
@@ -67,7 +68,7 @@ def tile_list_porter_dispatch_memory_kernel(tc, tab_words, tab_scales, offs, off
         wgs_dealt = [sb([P, S], F32, "wgs_dealt%d" % u) for u in range(2)]
         wgo_t = sb([P, WATCHED], F32, "wgo_t")
         jobs_t = sb([P, NTILES, WATCHED], F32, "jobs_t")
-        handsets = [sb([P, T2], F32, "handset%d" % i) for i in range(2)]
+        handsets = [sb([P, T2], F32, "handset0")]
 
         nc.gpsimd.memset(warm[:], 0.0)
         nc.gpsimd.memset(gain_rows[:], 0.0)
@@ -78,7 +79,6 @@ def tile_list_porter_dispatch_memory_kernel(tc, tab_words, tab_scales, offs, off
         nc.vector.memset(pages[1][:], 0.0)
         nc.vector.memset(pages[2][:], 0.0)
         nc.vector.memset(handsets[0][:], 0.0)
-        nc.vector.memset(handsets[1][:], 0.0)
 
         wa_k = wa.rearrange("(p j) r -> p j r", j=4)
 
@@ -244,7 +244,10 @@ def tile_list_porter_dispatch_memory_kernel(tc, tab_words, tab_scales, offs, off
                 nc.tensor.transpose(bank[LAST_BANKS[quarter]][:, P * t:P * (t + 1)], words[:, P * block:P * (block + 1)], ident[:])
 
         def turn_back(b, h):
-            z_in[b, h] = sb([P, 4 * BANK], BF16, "z_in%d%d" % (b, h))
+            if (b, h) == (1, 1):
+                z_in[b, h] = laid.tile([P, 4 * BANK], BF16, name="z_in11", offset=4096, align_bytes=256)
+            else:
+                z_in[b, h] = sb([P, 4 * BANK], BF16, "z_in%d%d" % (b, h))
             if b == 1:
                 z_w[b, h] = sb([P, BANK], U32, "z_w%d%d" % (b, h))
             for g in range(2):
@@ -379,11 +382,15 @@ def tile_list_porter_dispatch_memory_kernel(tc, tab_words, tab_scales, offs, off
         quantise_back(1, 0, 1, back_second[:])
         sum_slice(LAST, expected_part=False)
         turn_early(3)
+        back_gap = sb([P, 2 * P], U32, "back_gap", "z_early1")
+        quantise_back(0, 2, NTILES, back_gap[:])
         turn_back(1, 0)
         turn_back(1, 1)
-        back_rest = sb([P, 2, K - P], U32, "back_rest", "z_in11")
-        for b in range(2):
-            quantise_back(b, 1, NTILES, back_rest[:, b, :])
+        back_rest = laid.tile([P, K], U32, name="back_rest", offset=4096, align_bytes=256)
+        quantise_back(0, 1, 2, back_rest[:, 0:P])
+        quantise_back(1, 1, NTILES, back_rest[:, P:K])
+        handsets.append(laid.tile([P, T2], F32, name="handset1", offset=4096 + 3840, align_bytes=256))
+        nc.vector.memset(handsets[1][:], 0.0)
         y = [sb([P, T2], F32, "y%d" % s, "exp%d" % s) for s in range(NTILES)]
         x = {}
 

from contextlib import ExitStack

import concourse.mybir as mybir
from concourse.masks import make_identity

K, H, T, S, T2, WATCHED = 512, 1024, 2048, 512, 1024, 512
FLOPS = 2 * (K * H * S + 2 * H * K * T2)

F32 = mybir.dt.float32
BF16 = mybir.dt.bfloat16
I32 = mybir.dt.int32
U32 = mybir.dt.uint32
U16 = mybir.dt.uint16
U8 = mybir.dt.uint8
FP8X4 = mybir.dt.float8_e4m3fn_x4
FP4X4 = mybir.dt.float4_e2m1fn_x4
MULT = mybir.AluOpType.mult
ADD = mybir.AluOpType.add
COPY = mybir.ActivationFunctionType.Copy
SIGMOID = mybir.ActivationFunctionType.Sigmoid

P = 128
BANK = 512
HALF_LIST = 256
FIRST = 128
QUARTER = 256
SLICES, NTILES = H // P, K // P
LAST = SLICES - 1
PAGES = 3
WA_PIECES = [(0, 1), (1, 2), (2, 4), (4, 6), (6, 8)]
WA_CODES = [(0, 1), (1, 2), (2, 4), (4, 5), (5, 8)]
Y_BANKS = [(2, 5), (6, 7), (1, 3), (4, 2)]
ENCODE_BANKS = [0, 2, 3, 0, 1, 2, 3, 2]
LAST_BANKS = [6, 7, 3, 4]


def tile_list_porter_dispatch_memory_kernel(tc, tab_words, tab_scales, offs, offs2, offs3, offs4, wa, gin, gup,
                                                      wgs, expected, w4_words, w4_scales, gout, jobs, wgo, out):
    nc = tc.nc
    with ExitStack() as ctx:
        keep = ctx.enter_context(tc.tile_pool(name="keep", bufs=1))
        laid = ctx.enter_context(tc.tile_pool(name="laid", bufs=1))
        psum = ctx.enter_context(tc.psum_pool(name="psum", bufs=1))
        bank = [psum.tile([P, BANK], F32, name="bank%d" % i) for i in range(8)]

        def sb(shape, dt, name, tag=None):
            return keep.tile(shape, dt, name=name, tag=tag or name, align_bytes=256)

        lists = [keep.tile([P, S // 16], U16, name="list%d" % i) for i in range(4)]
        tab_w = sb([P, T], U32, "tab_w")
        tab_s = sb([P, T], U8, "tab_s")
        w4_w = sb([P, 2, 2 * K], U8, "w4_w")
        gain_rows = sb([P, 2 * P], F32, "gain_rows")
        gain_dealt = sb([P, 2 * P], F32, "gain_dealt")
        gout_loaded = sb([P, NTILES], F32, "gout_loaded")
        gout_cols = sb([P, 8], F32, "gout_cols")
        gout_last = sb([P, 8], F32, "gout_last")
        gout_first = sb([P, 8], F32, "gout_first")
        gin_first = [sb([P, 8], F32, "gin_first%d" % h) for h in range(2)]
        gin_cols = sb([P, 4, 4], F32, "gin_cols")
        gup_cols = sb([P, 4, 4], F32, "gup_cols")
        ident = sb([P, P], F32, "ident")
        warm = sb([P, 8], F32, "warm")
        pages = [sb([P, T2], F32, "page%d" % i) for i in range(PAGES)]
        wa_by_k = [sb([P, 4, P * (b - a)], F32, "wa_by_k%d" % i) for i, (a, b) in enumerate(WA_PIECES)]
        exp_t = [sb([P, T2], F32, "exp%d" % s) for s in range(SLICES)]
        wgs_t = sb([P, S], F32, "wgs_t")
        wgs_dealt = [sb([P, S], F32, "wgs_dealt%d" % u) for u in range(2)]
        wgo_t = sb([P, WATCHED], F32, "wgo_t")
        jobs_t = sb([P, NTILES, WATCHED], F32, "jobs_t")
        handsets = [sb([P, T2], F32, "handset0")]

        nc.gpsimd.memset(warm[:], 0.0)
        nc.gpsimd.memset(gain_rows[:], 0.0)
        nc.gpsimd.memset(tab_s[:].bitcast(U32), 0)
        nc.gpsimd.memset(ident[:], 0.0)
        make_identity(nc, ident[:], nomemset=True)
        nc.vector.memset(pages[0][:], 0.0)
        nc.vector.memset(pages[1][:], 0.0)
        nc.vector.memset(pages[2][:], 0.0)
        nc.vector.memset(handsets[0][:], 0.0)

        wa_k = wa.rearrange("(p j) r -> p j r", j=4)

        def load_wa_by_k(i):
            a, b = WA_PIECES[i]
            nc.sync.dma_start(out=wa_by_k[i][:], in_=wa_k[:, :, P * a:P * b])

        def load_expected(s):
            if s < 4:
                nc.sync.dma_start(out=exp_t[s][:], in_=expected[P * s:P * (s + 1), :])
            else:
                u, half = divmod(s - 4, 2)
                rows = expected[BANK + 2 * P * half:BANK + 2 * P * (half + 1), :]
                nc.sync.dma_start(out=exp_t[s][:], in_=rows.rearrange("(a u e) t -> u a e t", u=2, e=2)[u])

        def load_wgs_dealt(u):
            for half in range(2):
                nc.sync.dma_start(out=wgs_dealt[u][64 * half:64 * (half + 1), :],
                                  in_=wgs.rearrange("(a u e) j -> u a e j", u=2, e=2)[u])

        nc.sync.dma_start(lists[0][:], offs)
        load_wa_by_k(0)
        nc.sync.dma_start(out=gain_rows[8:12, :], in_=gin.rearrange("(s p) -> s p", p=2 * P))
        nc.sync.dma_start(out=gain_rows[12:16, :], in_=gup.rearrange("(s p) -> s p", p=2 * P))
        for q in range(4):
            nc.sync.dma_start(out=tab_s[q:P:32, :].bitcast(I32), in_=tab_scales[0, q:16:4, :].bitcast(I32))
        nc.sync.dma_start(out=tab_w[:].bitcast(I32), in_=tab_words[0].rearrange("p t i -> p (t i)").bitcast(I32))
        nc.sync.dma_start(out=wgs_t[:], in_=wgs)
        nc.sync.dma_start(lists[1][:], offs2)
        load_wa_by_k(1)
        load_wa_by_k(2)
        load_expected(0)
        load_wa_by_k(3)
        load_expected(1)
        load_wa_by_k(4)
        load_expected(2)
        load_wgs_dealt(0)
        load_expected(3)
        v_s = sb([P, S], U8, "v_s")
        nc.vector.tensor_copy(v_s[:], tab_s[:].indirect(lists[0][:]))
        w4_s = sb([P, 2, K], U8, "w4_s", "tab_s")
        nc.sync.dma_start(out=w4_w[:].bitcast(I32), in_=w4_words.rearrange("a p c -> p a c").bitcast(I32))
        for q in range(4):
            nc.sync.dma_start(out=w4_s[32 * q:32 * q + 4, :, :].bitcast(I32),
                              in_=w4_scales[:, 4 * q:4 * q + 4, :].rearrange("a r c -> r a c").bitcast(I32))
        with nc.allow_non_contiguous_dma(reason="gout, one value a partition"):
            nc.sync.dma_start(out=gout_loaded[:], in_=gout.rearrange("(s p) -> p s", p=P))
        load_expected(4)
        load_wgs_dealt(1)
        load_expected(5)
        load_expected(6)
        load_expected(7)
        nc.sync.dma_start(lists[2][:], offs3)
        nc.sync.dma_start(lists[3][:], offs4)
        nc.sync.dma_start(out=jobs_t[:], in_=jobs.rearrange("(s p) m -> p s m", p=P))
        nc.sync.dma_start(out=wgo_t[:], in_=wgo)

        nc.scalar.activation(warm[:, 0:1], warm[:, 1:2], SIGMOID)

        nc.scalar.copy(gain_dealt[:].rearrange("s (u a e) -> s u a e", u=2, e=2),
                       gain_rows[:].rearrange("s (a u e) -> s u a e", u=2, e=2))
        for c in range(4):
            source = (gain_rows, gain_dealt)[c // 2]
            nc.tensor.transpose(bank[2][:, P * c:P * (c + 1)], source[:, P * (c % 2):P * (c % 2 + 1)], ident[:])
        turned_gains = bank[2][:].rearrange("p (c s) -> p c s", c=4)
        for h in range(2):
            nc.scalar.copy(gin_first[h][:, 0:1], turned_gains[:, 0, 8:9])
        nc.scalar.copy(gin_cols[:], turned_gains[:, :, 8:12])
        nc.scalar.activation(gup_cols[:], turned_gains[:, :, 12:16], COPY, scale=-1.0)

        def gain(cols, s):
            c, row = (s % 2, s // 2) if s < 4 else (2 + (s - 4) // 2, 2 + s % 2)
            return cols[:, c, row:row + 1]

        v_w = sb([P, S], U32, "v_w")
        wa_w = [sb([P, P * (b - a)], U32, "wa_w%d" % i) for i, (a, b) in enumerate(WA_CODES)]
        wa_s = [sb([P, P * (b - a)], U8, "wa_s%d" % i) for i, (a, b) in enumerate(WA_CODES)]
        grouped = [sb([P, 4 * BANK], BF16, "wa_grouped%d" % b) for b in range(2)]
        sig = {}
        weight = {}

        def group_wa(i):
            a, b = WA_PIECES[i]
            if a < 4:
                piece = grouped[0][:, 4 * P * a:4 * P * b]
                nc.scalar.copy(piece.rearrange("p (c i j) -> p c j i", i=4, j=4),
                               wa_by_k[i][:].rearrange("p j (c i) -> p c j i", i=4))
            else:
                half = (a - 4) // 2
                nc.scalar.copy(grouped[1][:].rearrange("p (u h a e j) -> p u h a j e", u=2, h=2, e=2, j=4)[:, :, half],
                               wa_by_k[i][:].rearrange("p j (a u e) -> p u a j e", u=2, e=2))

        def quantise_wa(i):
            a, b = WA_CODES[i]
            nc.vector.quantize_mx(out=wa_w[i][:].bitcast(FP8X4), scales=wa_s[i][:],
                                  in_=grouped[a // 4][:, 4 * P * (a % 4):4 * P * (a % 4 + b - a)])

        def encode(s, tag=None):
            i = [n for n, (a, b) in enumerate(WA_CODES) if a <= s < b][0]
            c = slice(P * (s - WA_CODES[i][0]), P * (s - WA_CODES[i][0] + 1))
            acc = bank[ENCODE_BANKS[s]]
            sig[s] = sb([P, S], F32, "sig%d" % s, tag)
            nc.tensor.matmul_mx(out=acc[:], lhsT=wa_w[i][:, c].bitcast(FP8X4), lhsT_scale=wa_s[i][:, c],
                                rhs=v_w[:].bitcast(FP8X4), rhs_scale=v_s[:], start=True, stop=True)
            nc.scalar.activation(sig[s][:], acc[:], SIGMOID, scale=gain(gin_cols, s))

        def make_weight(s, tag=None):
            weight[s] = sb([P, S], F32, "weight%d" % s, tag)
            rows = wgs_t if s < 4 else wgs_dealt[(s - 4) // 2]
            nc.scalar.activation(weight[s][:], rows[:], COPY, scale=gain(gup_cols, s))

        def place(s):
            nc.vector.tensor_tensor(pages[s % PAGES][:].indirect(lists[1][:]), sig[s][:], weight[s][:], MULT)

        halves0 = [sb([P, 8 * QUARTER], BF16, "z_t0%d" % h) for h in range(2)]
        early1 = [sb([P, 4 * QUARTER], BF16, "z_early%d" % h) for h in range(2)]
        late1 = [sb([P, 2 * QUARTER], BF16, "z_late%d" % q) for q in range(4)]
        z_w = {}
        z_s = [[sb([P, BANK], U8, "z_s%d%d" % (b, h)) for h in range(2)] for b in range(2)]
        back_in = [sb([P, 4 * K], BF16, "back_in%d" % b) for b in range(2)]
        back_s = [sb([P, K], U8, "back_s%d" % b) for b in range(2)]
        back_w = {}

        def sum_slice(s, expected_part=True, page_part=True):
            page = pages[s % PAGES]
            b, in_pass = divmod(s, 4)
            rows = slice(32 * in_pass, 32 * in_pass + 32)
            blocks = 4
            banks = [0, 1] if s == LAST else [4 + 2 * (s % 2), 5 + 2 * (s % 2)]
            for i, bk in enumerate(banks if expected_part else []):
                for tb in range(blocks):
                    c = slice(P * (blocks * i + tb), P * (blocks * i + tb + 1))
                    nc.tensor.matmul(bank[bk][:, P * tb:P * (tb + 1)], exp_t[s][:, c], ident[:],
                                     start=(tb == 0), stop=False, is_transpose=True)
            for i, bk in enumerate(banks if page_part else []):
                for tb in range(blocks):
                    c = slice(P * (blocks * i + tb), P * (blocks * i + tb + 1))
                    nc.tensor.matmul(bank[bk][:, P * tb:P * (tb + 1)], page[:, c], ident[:],
                                     start=False, stop=(tb == blocks - 1), is_transpose=True)
                if b == 0:
                    dst = halves0[i][:].rearrange("c (g u t q e) -> c g u t q e", g=2, u=2, t=2, e=2)[:, :, :, :, rows, :]
                    nc.scalar.copy(dst, bank[bk][:].rearrange("c (g t q u e) -> c g u t q e", g=2, t=2, u=2, e=2))
                    continue
                u, half = divmod(in_pass, 2)
                if u == 0:
                    nc.scalar.copy(early1[i][:].rearrange("c (t h p) -> c t h p", t=4, h=2)[:, :, half, :],
                                   bank[bk][:].rearrange("c (t p) -> c t p", t=4))
                    continue
                for g in range(blocks // 2):
                    dst = late1[2 * i + g][:].rearrange("c (t h p) -> c t h p", t=2, h=2)[:, :, half, :]
                    src = bank[bk][:, QUARTER * g:QUARTER * (g + 1)].rearrange("c (t p) -> c t p", t=2)
                    if s == LAST and i == 1:
                        nc.vector.tensor_copy(dst, src)
                    else:
                        nc.scalar.copy(dst, src)

        z_in = {}

        def turn_early(quarter):
            words = early1[quarter // 2][:].bitcast(F32)
            for t in range(2):
                block = 2 * (quarter % 2) + t
                nc.tensor.transpose(bank[LAST_BANKS[quarter]][:, P * t:P * (t + 1)], words[:, P * block:P * (block + 1)], ident[:])

        def turn_back(b, h):
            if (b, h) == (1, 1):
                z_in[b, h] = laid.tile([P, 4 * BANK], BF16, name="z_in11", offset=4096, align_bytes=256)
            else:
                z_in[b, h] = sb([P, 4 * BANK], BF16, "z_in%d%d" % (b, h))
            if b == 1:
                z_w[b, h] = sb([P, BANK], U32, "z_w%d%d" % (b, h))
            for g in range(2):
                quarter = 2 * h + g
                acc = bank[LAST_BANKS[quarter] if b == 1 else g]
                if b == 0:
                    words = halves0[h][:].bitcast(F32)[:, BANK * g:BANK * (g + 1)]
                    for j in range(4):
                        nc.tensor.transpose(acc[:, P * j:P * (j + 1)], words[:, P * j:P * (j + 1)], ident[:])
                else:
                    words = late1[quarter][:].bitcast(F32)
                    for t in range(2):
                        nc.tensor.transpose(acc[:, P * (2 + t):P * (3 + t)], words[:, P * t:P * (t + 1)], ident[:])
                dst = z_in[b, h][:].bitcast(F32)[:, BANK * g:BANK * (g + 1)].rearrange("p (c u) -> p c u", u=2)
                src = acc[:].rearrange("p (u c) -> p c u", u=2)
                if b == 1 and quarter == 1:
                    nc.vector.tensor_copy(dst, src)
                else:
                    nc.scalar.copy(dst, src)
                if b == 1:
                    c = slice(QUARTER * g, QUARTER * (g + 1))
                    nc.vector.quantize_mx(out=z_w[b, h][:, c].bitcast(FP8X4), scales=z_s[b][h][:, c],
                                          in_=z_in[b, h][:, 4 * QUARTER * g:4 * QUARTER * (g + 1)])

        def quantise_z0(h, tag=None):
            z_w[0, h] = sb([P, BANK], U32, "z_w0%d" % h, tag)
            nc.vector.quantize_mx(out=z_w[0, h][:].bitcast(FP8X4), scales=z_s[0][h][:], in_=z_in[0, h][:])

        def turn_wa(b, jj, bk):
            words = grouped[b][:].bitcast(F32)
            acc = bank[bk]
            for i in range(4):
                if b == 0:
                    rows = words[:, 2 * i + jj:2 * BANK:8]
                else:
                    rows = words[:, BANK * (i // 2) + 2 * (i % 2) + jj:BANK * (i // 2 + 1):4]
                nc.tensor.transpose(acc[:, P * i:P * (i + 1)], rows, ident[:])
            dst = back_in[b][:].rearrange("q (p jj e i) -> q p jj i e", jj=2, e=2, i=4)[:, :, jj, :, :]
            nc.scalar.copy(dst, acc[:].bitcast(BF16).rearrange("q (i p e) -> q p i e", i=4, e=2))

        def quantise_back(b, first, last, codes):
            nc.vector.quantize_mx(out=codes.bitcast(FP8X4), scales=back_s[b][:, P * first:P * last],
                                  in_=back_in[b][:, 4 * P * first:4 * P * last])
            for s in range(first, last):
                back_w[b, s] = codes[:, P * (s - first):P * (s - first + 1)]

        def y_bank(s, h, g):
            return bank[0] if (s, h, g) == (0, 1, 1) else bank[Y_BANKS[s][h]]

        def project(s, b, h, g=None, alone=True):
            first, width = (0, BANK) if g is None else (QUARTER * g, QUARTER)
            at = 0 if alone else first
            acc = y_bank(s, h, g)[:, at:at + width]
            c = slice(P * s, P * (s + 1))
            t = slice(first, first + width)
            nc.tensor.matmul_mx(out=acc, lhsT=back_w[b, s].bitcast(FP8X4), lhsT_scale=back_s[b][:, c],
                                rhs=z_w[b, h][:, t].bitcast(FP8X4), rhs_scale=z_s[b][h][:, t], start=(b == 0), stop=False)
            nc.tensor.matmul_mx(out=acc, lhsT=w4_w[:, b, 2 * P * s:2 * P * (s + 1)].bitcast(FP4X4),
                                lhsT_scale=w4_s[:, b, c], rhs=z_w[b, h][:, t].bitcast(FP8X4), rhs_scale=z_s[b][h][:, t],
                                start=False, stop=(b == 1 and (alone or g == 1)))

        group_wa(0)
        quantise_wa(0)
        pieces = [(0, FIRST), (FIRST, S)]
        for h, (a, b) in enumerate(pieces):
            nc.vector.tensor_copy(v_w[:, a:b], tab_w[:].indirect(lists[0][:, a // 16:b // 16]))
            for c in ([slice(0, FIRST)], [slice(FIRST, 2 * FIRST), slice(2 * FIRST, S)])[h]:
                nc.tensor.matmul_mx(out=bank[h][:, c], lhsT=wa_w[0][:].bitcast(FP8X4), lhsT_scale=wa_s[0][:],
                                    rhs=v_w[:, c].bitcast(FP8X4), rhs_scale=v_s[:, c], start=True, stop=True)
        weight[0] = sb([P, S], F32, "weight0")
        nc.vector.tensor_scalar(weight[0][:], wgs_t[:], gain(gup_cols, 0), None, MULT)
        for h, (a, b) in enumerate(pieces):
            if h == 1:
                weight[1] = sb([P, S], F32, "weight1", "gin_first0")
                nc.vector.tensor_scalar(weight[1][:], wgs_t[:], gain(gup_cols, 1), None, MULT)
                group_wa(1)
                quantise_wa(1)
            sig0 = sb([P, b - a], F32, "sig0_%d" % h, (None, "wa_by_k1")[h])
            nc.scalar.activation(sig0[:], bank[h][:, a:b], SIGMOID, scale=gin_first[h][:, 0:1])
            nc.vector.tensor_tensor(pages[0][:].indirect(lists[1][:, a // 16:b // 16]), sig0[:], weight[0][:, a:b], MULT)
        group_wa(2)
        quantise_wa(2)
        encode(1, "wa_by_k2")
        place(1)
        encode(2)
        make_weight(2, "gin_first1")
        place(2)
        group_wa(3)
        quantise_wa(3)
        sum_slice(0)
        encode(3)
        make_weight(3, "wa_by_k3")
        place(3)
        group_wa(4)
        quantise_wa(4)
        sum_slice(1)
        encode(4)
        make_weight(4, "wa_by_k4")
        place(4)
        turn_wa(0, 0, 0)
        sum_slice(2)
        encode(5)
        make_weight(5)
        place(5)
        nc.scalar.activation(gout_cols[:, 1:NTILES - 1], gout_loaded[:, 1:NTILES - 1], COPY, scale=-1.0)
        nc.scalar.activation(gout_first[:, 0:1], gout_loaded[:, 0:1], COPY, scale=-1.0)
        nc.scalar.activation(gout_last[:, 0:1], gout_loaded[:, NTILES - 1:NTILES], COPY, scale=-1.0)
        turn_wa(0, 1, 1)
        back_first = sb([P, P], U32, "back_first")
        quantise_back(0, 0, 1, back_first[:])
        sum_slice(3)
        turn_back(0, 0)
        quantise_z0(0)
        encode(6)
        make_weight(6, "z_t00")
        place(6)
        turn_back(0, 1)
        turn_wa(1, 0, 0)
        sum_slice(4)
        encode(LAST)
        make_weight(LAST)
        place(LAST)
        sum_slice(5)
        turn_wa(1, 1, 3)
        sum_slice(LAST, page_part=False)
        sum_slice(6)
        project(0, 0, 0)
        for quarter in range(3):
            turn_early(quarter)
        quantise_z0(1, "z_early0")
        back_second = sb([P, P], U32, "back_second")
        quantise_back(1, 0, 1, back_second[:])
        sum_slice(LAST, expected_part=False)
        turn_early(3)
        back_gap = sb([P, 2 * P], U32, "back_gap", "z_early1")
        quantise_back(0, 2, NTILES, back_gap[:])
        turn_back(1, 0)
        turn_back(1, 1)
        back_rest = laid.tile([P, K], U32, name="back_rest", offset=4096, align_bytes=256)
        quantise_back(0, 1, 2, back_rest[:, 0:P])
        quantise_back(1, 1, NTILES, back_rest[:, P:K])
        handsets.append(laid.tile([P, T2], F32, name="handset1", offset=4096 + 3840, align_bytes=256))
        nc.vector.memset(handsets[1][:], 0.0)
        y = [sb([P, T2], F32, "y%d" % s, "exp%d" % s) for s in range(NTILES)]
        x = {}

        def bring_y(s, h, g=None):
            first, width = (0, BANK) if g is None else (QUARTER * g, QUARTER)
            column = {0: gout_first[:, 0:1], NTILES - 1: gout_last[:, 0:1]}.get(s, gout_cols[:, s:s + 1])
            dst, src = y[s][:, BANK * h + first:BANK * h + first + width], y_bank(s, h, g)[:, 0:width]
            nc.scalar.activation(dst, src, COPY, scale=column)

        def pick(s, tag=None):
            x[s] = sb([P, WATCHED], F32, "x%d" % s, tag)
            nc.vector.tensor_tensor(x[s][:], y[s][:].indirect(lists[2][:]), jobs_t[:, s, :], ADD)

        def hand_out(s):
            handset = handsets[s % 2]
            nc.vector.tensor_tensor(handset[:].indirect(lists[3][:]), x[s][:], wgo_t[:], MULT)
            nc.sync.dma_start(out=out[P * s:P * (s + 1), :], in_=handset[:])

        for g in range(2):
            project(0, 0, 1, g)
        for g in range(2):
            project(0, 1, 0, g, alone=False)
        bring_y(0, 0)
        for g in range(2):
            project(0, 1, 1, g)
            bring_y(0, 1, g)
        for s in range(1, NTILES):
            for h in range(2):
                project(s, 0, h)
                project(s, 1, h)
                bring_y(s, h)
        wgo_late = sb([P, HALF_LIST], F32, "wgo_late", "gout_first")
        nc.sync.dma_start(out=wgo_late[:], in_=wgo[:, HALF_LIST:WATCHED])
        x0 = [sb([P, HALF_LIST], F32, "x0_%d" % h) for h in range(2)]
        for h in range(2):
            nc.vector.tensor_tensor(x0[h][:], y[0][:].indirect(lists[2][:, 16 * h:16 * (h + 1)]),
                                    jobs_t[:, 0, HALF_LIST * h:HALF_LIST * (h + 1)], ADD)
        nc.vector.tensor_tensor(handsets[0][:].indirect(lists[3][:, 0:16]), x0[0][:], wgo_t[:, 0:HALF_LIST], MULT)
        pick(1)
        nc.vector.tensor_tensor(handsets[0][:].indirect(lists[3][:, 16:32]), x0[1][:], wgo_late[:], MULT)
        nc.sync.dma_start(out=out[0:P, :], in_=handsets[0][:])
        hand_out(1)
        pick(2, "gout_last")
        pick(3)
        hand_out(2)
        hand_out(3)
